import numpy as np
import ml_dtypes


def mxq(x, axis, fmt="e4m3"):
    dtype, down = {"e4m3": (ml_dtypes.float8_e4m3fn, 7), "e5m2": (ml_dtypes.float8_e5m2, 14)}[fmt]
    v = np.moveaxis(np.asarray(x, np.float32).astype(ml_dtypes.bfloat16).astype(np.float64), axis, -1)
    blocks = v.reshape(v.shape[:-1] + (-1, 32))
    amax = np.abs(blocks).max(-1, keepdims=True)
    byte = np.maximum(np.where(amax > 0, np.frexp(amax)[1] - 1 + 127, 0) - down, 1)
    scale = np.exp2(byte - 127.0)
    codes = (blocks / scale).astype(np.float32).astype(dtype).astype(np.float64)
    return np.moveaxis((codes * scale).reshape(v.shape), -1, axis)


WIDE = False


def mx_kscale(k):
    if not WIDE:
        return np.ones(k)
    levels = np.array([10, -10, 5, -5, 0])
    if k % 512:
        return np.exp2(np.random.permutation(np.resize(levels, k // 32))).repeat(32)
    a = np.empty((k // 512, 16))
    for p in range(k // 512):
        a[p, :8] = np.random.permutation(np.resize(levels, 8))
        for g in range(8):
            far = levels[np.abs(levels - a[p, g]) >= 10]
            a[p, g + 8] = far[np.random.randint(len(far))]
    return np.exp2(a.ravel()).repeat(32)


def f64(x):
    return np.asarray(x).astype(np.float64)


def striped8(idx):
    return np.concatenate([v.reshape(-1, 16).T for v in idx]).astype(np.uint16)


def unstriped8(offs):
    return np.stack([offs[16 * g:16 * g + 16].T.reshape(-1) for g in range(8)]).astype(np.int64)


E2M1 = np.array([0.0, 0.5, 1.0, 1.5, 2.0, 3.0, 4.0, 6.0, -0.0, -0.5, -1.0, -1.5, -2.0, -3.0, -4.0, -6.0])


def pack_weight(w, fmt):
    k, n = w.shape
    w = f64(np.asarray(w, np.float32).astype(ml_dtypes.bfloat16)).reshape(k // 32, 32, n)
    amax = np.abs(w).max(1)
    if fmt == "e4m3":
        byte = np.frexp(amax)[1] - 1 + 127 - 7
    else:
        mant, ex = np.frexp(amax / 6.0)
        byte = np.where(mant > 0.5, ex, ex - 1) + 127
    byte = np.clip(np.where(amax > 0, byte, 1), 1, 254)
    scaled = (w * np.exp2(127.0 - byte)[:, None, :]).reshape(k, n).astype(np.float32)
    by_word = np.ascontiguousarray(scaled.reshape(k // 512, 128, 4, n).transpose(0, 1, 3, 2))
    if fmt == "e4m3":
        words = by_word.astype(ml_dtypes.float8_e4m3fn).view(np.uint8)
    else:
        c = by_word.astype(ml_dtypes.float4_e2m1fn).view(np.uint8) & 0xF
        words = (c[..., 0::2] | (c[..., 1::2] << 4)).reshape(k // 512, 128, 2 * n)
    return np.ascontiguousarray(words), np.ascontiguousarray(byte.astype(np.uint8).reshape(k // 512, 16, n))


def unpack_weight(words, scales, fmt):
    g, _, n = scales.shape
    words = np.ascontiguousarray(words).reshape(g, 128, n, -1)
    if fmt == "e4m3":
        vals = words.view(ml_dtypes.float8_e4m3fn).astype(np.float64)
    else:
        nib = np.empty((g, 128, n, 4), np.uint8)
        nib[..., 0::2] = words & 0xF
        nib[..., 1::2] = words >> 4
        vals = E2M1[nib]
    vals = vals * np.repeat(np.exp2(scales.astype(np.float64) - 127.0), 8, axis=1)[..., None]
    return vals.transpose(0, 1, 3, 2).reshape(g * 512, n)


def silu(v):
    return v / (1.0 + np.exp(-np.maximum(v, -700.0)))


K, M, T, S = 1024, 1024, 1024, 512


def setup_inputs():
    n = np.random.standard_normal
    s = mx_kscale(K)[:, None]
    p_w = pack_weight(n((K, M)) / np.sqrt(K) / s, "e4m3")
    return {
        "xT": (n((K, T)) * s).astype(np.float32),
        "w_words": p_w[0],
        "w_scales": p_w[1],
        "wgt": np.repeat(np.random.uniform(0.5, 2.0, (8, S)), 16, axis=0).astype(np.float32),
        "b": (0.3 * n(1024)).astype(np.float32),
        "wgo": np.repeat(np.random.uniform(0.5, 2.0, (8, S)), 16, axis=0).astype(np.float32),
        "offs": striped8(np.stack([np.random.permutation(T)[:S] for _ in range(8)])),
        "offs2": striped8(np.stack([np.random.permutation(T)[:S] for _ in range(8)])),
    }


def reference(xT, w_words, w_scales, wgt, b, wgo, offs, offs2):
    idx = unstriped8(offs)
    group = np.arange(K) % 512 // 64
    xg = f64(wgt)[np.arange(K) // 4 % 128] * f64(xT)[np.arange(K)[:, None], idx[group]]
    xT_ = mxq(xg, 0, "e4m3")
    w_ = unpack_weight(w_words, w_scales, "e4m3")
    y = w_.T @ xT_
    place = unstriped8(offs2)[np.arange(M) % 128 // 16]
    out = np.zeros((M, T))
    out[np.arange(M)[:, None], place] = f64(wgo)[np.arange(M) % 128] * (silu(y + f64(b)[:, None]))
    return out

@@ -1,0 +1,168 @@
+from contextlib import ExitStack
+
+import concourse.mybir as mybir
+from concourse.masks import make_identity
+
+K, M, T, S = 1024, 1024, 1024, 512
+FLOPS = 2 * K * M * S
+
+P = 128
+PACK = 4
+PASSES = K // (P * PACK)
+ROW_TILES = M // P
+HALVES = 2
+SH = S // HALVES
+OH = SH // 16
+VECTOR_SHARE = 176
+WINDOWS = 4
+
+F32 = mybir.dt.float32
+BF16 = mybir.dt.bfloat16
+I32 = mybir.dt.int32
+U32 = mybir.dt.uint32
+U16 = mybir.dt.uint16
+U8 = mybir.dt.uint8
+FP8X4 = mybir.dt.float8_e4m3fn_x4
+MULT = mybir.AluOpType.mult
+SILU = mybir.ActivationFunctionType.Silu
+
+
+def tile_list_hboth_silu_kernel(tc, xT, w_words, w_scales, wgt, b, wgo, offs, offs2, out):
+    nc = tc.nc
+    with ExitStack() as ctx:
+        keep = ctx.enter_context(tc.tile_pool(name="keep", bufs=1))
+        ypool = ctx.enter_context(tc.tile_pool(name="ypool", bufs=16))
+        psum = ctx.enter_context(tc.psum_pool(name="psum", bufs=8))
+
+        offs_sb = keep.tile([P, S // 16], U16, name="offs_sb")
+        offs2_sb = keep.tile([P, S // 16], U16, name="offs2_sb")
+        wgt_sb = [keep.tile([P, SH], F32, name=f"wgt{h}") for h in range(HALVES)]
+        wgo_sb = [keep.tile([P, SH], F32, name=f"wgo{h}") for h in range(HALVES)]
+        x_sb = [[keep.tile([P, T], F32, name=f"x{a}_{i}") for i in range(PACK)] for a in range(PASSES)]
+        g_sb = [[keep.tile([P, PACK, SH], F32, name=f"g{a}_{h}") for h in range(HALVES)] for a in range(PASSES)]
+        xb_sb = [[keep.tile([P, SH, PACK], BF16, name=f"xb{a}_{h}", align_bytes=64) for h in range(HALVES)] for a in range(PASSES)]
+        xq_sb = [[keep.tile([P, SH], U32, name=f"xq{a}_{h}", align_bytes=64) for h in range(HALVES)] for a in range(PASSES)]
+        xs_sb = [[keep.tile([P, SH], U8, name=f"xs{a}_{h}", align_bytes=64) for h in range(HALVES)] for a in range(PASSES)]
+        w_sb = [keep.tile([P, PASSES, M // 2], I32, name=f"w{c}", align_bytes=64) for c in range(2)]
+        ws_sb = keep.tile([P, M], U8, name="ws_sb", align_bytes=64)
+        win_sb = [keep.tile([P, T], F32, name=f"win{r}") for r in range(WINDOWS)]
+        brow = keep.tile([P, P], F32, name="brow")
+        ident = keep.tile([P, P], F32, name="ident")
+        bcol = keep.tile([P, ROW_TILES], F32, name="bcol")
+        warm = keep.tile([P, 1], F32, name="warm")
+
+        x_view = xT.rearrange("(a p i) t -> a i p t", p=P, i=PACK)
+        w_view = w_words.rearrange("a p n t -> p a (n t)")
+
+        def load_w(c):
+            nc.sync.dma_start(out=w_sb[c][:], in_=w_view[:, :, c * 2 * M : (c + 1) * 2 * M].bitcast(I32))
+
+        nc.sync.dma_start(offs_sb[:], offs)
+        nc.sync.dma_start(out=wgt_sb[0][:], in_=wgt[:, 0:SH])
+        nc.sync.dma_start(out=x_sb[0][0][:], in_=x_view[0, 0])
+        nc.sync.dma_start(out=wgt_sb[1][:], in_=wgt[:, SH:S])
+        for a in range(PASSES):
+            for i in range(PACK):
+                if (a, i) != (0, 0):
+                    nc.sync.dma_start(out=x_sb[a][i][:], in_=x_view[a, i])
+        load_w(0)
+        nc.sync.dma_start(offs2_sb[:], offs2)
+        nc.sync.dma_start(out=wgo_sb[0][:], in_=wgo[:, 0:SH])
+        load_w(1)
+        nc.sync.dma_start(out=wgo_sb[1][:], in_=wgo[:, SH:S])
+
+        nc.gpsimd.memset(warm[:], 0.0)
+        nc.scalar.activation(warm[:], warm[:], SILU)
+        make_identity(nc, ident[:])
+        nc.gpsimd.memset(brow[:], 0.0)
+        nc.gpsimd.memset(ws_sb[:].bitcast(I32), 0)
+        for q in range(4):
+            nc.gpsimd.dma_start(
+                out=ws_sb[32 * q : 32 * q + 8, :].bitcast(I32),
+                in_=w_scales[:, 4 * q : 4 * q + 4, :].bitcast(I32),
+            )
+        nc.gpsimd.dma_start(out=brow[0:ROW_TILES, :], in_=b.rearrange("(r p) -> r p", p=P))
+
+        for w in range(WINDOWS):
+            nc.vector.memset(win_sb[w][:].bitcast(I32), 0)
+
+        bank = psum.tile([P, P], F32, name="bank")
+        nc.tensor.transpose(bank[:], brow[:], ident[:])
+        nc.scalar.copy(bcol[:], bank[:, 0:ROW_TILES])
+
+        def gather(a, i, h):
+            nc.vector.tensor_tensor(
+                g_sb[a][h][:, i, :],
+                x_sb[a][i][:].indirect(offs_sb[:, h * OH : (h + 1) * OH]),
+                wgt_sb[h][:],
+                MULT,
+            )
+
+        def interleave(a, h):
+            nc.scalar.copy(
+                xb_sb[a][h][:].rearrange("p (c e) i -> p c i e", e=4),
+                g_sb[a][h][:].rearrange("p i (c e) -> p c i e", e=4),
+            )
+
+        def interleave_shared(a, h):
+            for engine_copy, part in ((nc.vector.tensor_copy, slice(0, VECTOR_SHARE)), (nc.scalar.copy, slice(VECTOR_SHARE, SH))):
+                engine_copy(
+                    xb_sb[a][h][:, part, :].rearrange("p (c e) i -> p c i e", e=4),
+                    g_sb[a][h][:, :, part].rearrange("p i (c e) -> p c i e", e=4),
+                )
+
+        def quantize(a, h):
+            nc.vector.quantize_mx(
+                out=xq_sb[a][h][:].bitcast(FP8X4),
+                scales=xs_sb[a][h][:],
+                in_=xb_sb[a][h][:].rearrange("p s i -> p (s i)"),
+            )
+
+        def multiply(r, h):
+            acc = psum.tile([P, SH], F32, name="bank")
+            c, col = divmod(r * P, M // 2)
+            for a in range(PASSES):
+                nc.tensor.matmul_mx(
+                    out=acc[:],
+                    lhsT=w_sb[c][:, a, col : col + P].bitcast(FP8X4),
+                    lhsT_scale=ws_sb[4 * a : P, r * P : (r + 1) * P],
+                    rhs=xq_sb[a][h][:].bitcast(FP8X4),
+                    rhs_scale=xs_sb[a][h][:],
+                    start=(a == 0),
+                    stop=(a == PASSES - 1),
+                )
+            y = ypool.tile([P, SH], F32, name="y")
+            nc.scalar.activation(y[:], acc[:], SILU, bias=bcol[:, r : r + 1])
+            return y
+
+        def scatter(r, h, y):
+            nc.vector.tensor_tensor(
+                win_sb[r % WINDOWS][:].indirect(offs2_sb[:, h * OH : (h + 1) * OH]), y[:], wgo_sb[h][:], MULT
+            )
+
+        for i in range(PACK):
+            for h in range(HALVES):
+                gather(0, i, h)
+        interleave(0, 0)
+        interleave(0, 1)
+        gather(1, 0, 0)
+        gather(1, 1, 0)
+        quantize(0, 0)
+        gather(1, 2, 0)
+        gather(1, 0, 1)
+        gather(1, 3, 0)
+        gather(1, 1, 1)
+        interleave_shared(1, 0)
+        quantize(0, 1)
+        quantize(1, 0)
+        gather(1, 2, 1)
+        gather(1, 3, 1)
+        for base in range(0, ROW_TILES, WINDOWS):
+            for h in range(HALVES):
+                for r in range(base, base + WINDOWS):
+                    scatter(r, h, multiply(r, h))
+                    if h == HALVES - 1:
+                        nc.sync.dma_start(out=out[r * P : (r + 1) * P, :], in_=win_sb[r % WINDOWS][:])
+                    if (r, h) == (1, 0):
+                        interleave(1, 1)
+                        quantize(1, 1)

@@ -10,11 +10,14 @@ P = 128
 PACK = 4
 PASSES = K // (P * PACK)
 ROW_TILES = M // P
-HALVES = 2
-SH = S // HALVES
-OH = SH // 16
-VECTOR_SHARE = 176
 WINDOWS = 4
+STAGED = 3
+PIECES = (slice(0, 128), slice(128, 256), slice(256, 512))
+FIRST = PIECES[0]
+REST = slice(128, 512)
+WHOLE = slice(0, S)
+PITCH = 768
+W_CHUNKS = (slice(0, 256), slice(256, 512), slice(512, 1024))
 
 F32 = mybir.dt.float32
 BF16 = mybir.dt.bfloat16
@@ -27,23 +30,36 @@ MULT = mybir.AluOpType.mult
 SILU = mybir.ActivationFunctionType.Silu
 
 
+def width(part):
+    return part.stop - part.start
+
+
+def columns(part):
+    return slice(part.start // 16, part.stop // 16)
+
+
 def tile_list_hboth_silu_kernel(tc, xT, w_words, w_scales, wgt, b, wgo, offs, offs2, out):
     nc = tc.nc
     with ExitStack() as ctx:
         keep = ctx.enter_context(tc.tile_pool(name="keep", bufs=1))
-        ypool = ctx.enter_context(tc.tile_pool(name="ypool", bufs=16))
         psum = ctx.enter_context(tc.psum_pool(name="psum", bufs=8))
 
         offs_sb = keep.tile([P, S // 16], U16, name="offs_sb")
         offs2_sb = keep.tile([P, S // 16], U16, name="offs2_sb")
-        wgt_sb = [keep.tile([P, SH], F32, name=f"wgt{h}") for h in range(HALVES)]
-        wgo_sb = [keep.tile([P, SH], F32, name=f"wgo{h}") for h in range(HALVES)]
+        wgo_sb = keep.tile([P, S], F32, name="wgo_sb")
         x_sb = [[keep.tile([P, T], F32, name=f"x{a}_{i}") for i in range(PACK)] for a in range(PASSES)]
-        g_sb = [[keep.tile([P, PACK, SH], F32, name=f"g{a}_{h}") for h in range(HALVES)] for a in range(PASSES)]
-        xb_sb = [[keep.tile([P, SH, PACK], BF16, name=f"xb{a}_{h}", align_bytes=64) for h in range(HALVES)] for a in range(PASSES)]
-        xq_sb = [[keep.tile([P, SH], U32, name=f"xq{a}_{h}", align_bytes=64) for h in range(HALVES)] for a in range(PASSES)]
-        xs_sb = [[keep.tile([P, SH], U8, name=f"xs{a}_{h}", align_bytes=64) for h in range(HALVES)] for a in range(PASSES)]
-        w_sb = [keep.tile([P, PASSES, M // 2], I32, name=f"w{c}", align_bytes=64) for c in range(2)]
+        g0 = keep.tile([P, PACK, S], F32, name="g0")
+        g1_first = keep.tile([P, PACK, width(FIRST)], F32, name="g1_first")
+        arena = keep.tile([P, PACK * PITCH], F32, name="arena", align_bytes=64)
+        g1_rest = arena[:].rearrange("p (i c) -> p i c", i=PACK)[:, :, 0 : width(REST)]
+        wgt_at = 2 * PITCH + width(REST) - width(FIRST)
+        wgt_sb = arena[:, wgt_at : wgt_at + S]
+        xb1_first = arena[:, 3 * PITCH : 3 * PITCH + 2 * width(FIRST)].bitcast(BF16).rearrange("p (s i) -> p s i", i=PACK)
+        xb0 = keep.tile([P, S, PACK], BF16, name="xb0", align_bytes=64)
+        xb1 = [xb1_first] + [keep.tile([P, width(c), PACK], BF16, name=f"xb1_{c.start}", align_bytes=64)[:] for c in PIECES[1:]]
+        xq_sb = [keep.tile([P, S], U32, name=f"xq{a}", align_bytes=64) for a in range(PASSES)]
+        xs_sb = [keep.tile([P, S], U8, name=f"xs{a}", align_bytes=64) for a in range(PASSES)]
+        w_sb = [keep.tile([P, PASSES, width(c)], I32, name=f"w{n}", align_bytes=64) for n, c in enumerate(W_CHUNKS)]
         ws_sb = keep.tile([P, M], U8, name="ws_sb", align_bytes=64)
         win_sb = [keep.tile([P, T], F32, name=f"win{r}") for r in range(WINDOWS)]
         brow = keep.tile([P, P], F32, name="brow")
@@ -54,22 +70,21 @@ def tile_list_hboth_silu_kernel(tc, xT, w_words, w_scales, wgt, b, wgo, offs, of
         x_view = xT.rearrange("(a p i) t -> a i p t", p=P, i=PACK)
         w_view = w_words.rearrange("a p n t -> p a (n t)")
 
-        def load_w(c):
-            nc.sync.dma_start(out=w_sb[c][:], in_=w_view[:, :, c * 2 * M : (c + 1) * 2 * M].bitcast(I32))
+        def load_w(n):
+            c = W_CHUNKS[n]
+            nc.sync.dma_start(out=w_sb[n][:], in_=w_view[:, :, PACK * c.start : PACK * c.stop].bitcast(I32))
 
         nc.sync.dma_start(offs_sb[:], offs)
-        nc.sync.dma_start(out=wgt_sb[0][:], in_=wgt[:, 0:SH])
-        nc.sync.dma_start(out=x_sb[0][0][:], in_=x_view[0, 0])
-        nc.sync.dma_start(out=wgt_sb[1][:], in_=wgt[:, SH:S])
+        nc.sync.dma_start(out=wgt_sb, in_=wgt)
         for a in range(PASSES):
             for i in range(PACK):
-                if (a, i) != (0, 0):
-                    nc.sync.dma_start(out=x_sb[a][i][:], in_=x_view[a, i])
+                nc.sync.dma_start(out=x_sb[a][i][:], in_=x_view[a, i])
         load_w(0)
         nc.sync.dma_start(offs2_sb[:], offs2)
-        nc.sync.dma_start(out=wgo_sb[0][:], in_=wgo[:, 0:SH])
+        nc.sync.dma_start(out=wgo_sb[:, FIRST], in_=wgo[:, FIRST])
         load_w(1)
-        nc.sync.dma_start(out=wgo_sb[1][:], in_=wgo[:, SH:S])
+        nc.sync.dma_start(out=wgo_sb[:, REST], in_=wgo[:, REST])
+        load_w(2)
 
         nc.gpsimd.memset(warm[:], 0.0)
         nc.scalar.activation(warm[:], warm[:], SILU)
@@ -90,79 +105,74 @@ def tile_list_hboth_silu_kernel(tc, xT, w_words, w_scales, wgt, b, wgo, offs, of
         nc.tensor.transpose(bank[:], brow[:], ident[:])
         nc.scalar.copy(bcol[:], bank[:, 0:ROW_TILES])
 
-        def gather(a, i, h):
-            nc.vector.tensor_tensor(
-                g_sb[a][h][:, i, :],
-                x_sb[a][i][:].indirect(offs_sb[:, h * OH : (h + 1) * OH]),
-                wgt_sb[h][:],
-                MULT,
-            )
+        def gather(dst, a, i, part):
+            nc.vector.tensor_tensor(dst, x_sb[a][i][:].indirect(offs_sb[:, columns(part)]), wgt_sb[:, part], MULT)
 
-        def interleave(a, h):
+        def rest_row(i):
+            return arena[:, i * PITCH : i * PITCH + width(REST)]
+
+        def interleave(dst, src):
             nc.scalar.copy(
-                xb_sb[a][h][:].rearrange("p (c e) i -> p c i e", e=4),
-                g_sb[a][h][:].rearrange("p i (c e) -> p c i e", e=4),
+                dst.rearrange("p (c e) i -> p c i e", e=4),
+                src.rearrange("p i (c e) -> p c i e", e=4),
             )
 
-        def interleave_shared(a, h):
-            for engine_copy, part in ((nc.vector.tensor_copy, slice(0, VECTOR_SHARE)), (nc.scalar.copy, slice(VECTOR_SHARE, SH))):
-                engine_copy(
-                    xb_sb[a][h][:, part, :].rearrange("p (c e) i -> p c i e", e=4),
-                    g_sb[a][h][:, :, part].rearrange("p i (c e) -> p c i e", e=4),
-                )
-
-        def quantize(a, h):
+        def quantize(a, part, src):
             nc.vector.quantize_mx(
-                out=xq_sb[a][h][:].bitcast(FP8X4),
-                scales=xs_sb[a][h][:],
-                in_=xb_sb[a][h][:].rearrange("p s i -> p (s i)"),
+                out=xq_sb[a][:, part].bitcast(FP8X4),
+                scales=xs_sb[a][:, part],
+                in_=src.rearrange("p s i -> p (s i)"),
             )
 
-        def multiply(r, h):
-            acc = psum.tile([P, SH], F32, name="bank")
-            c, col = divmod(r * P, M // 2)
+        def multiply(r, part):
+            acc = psum.tile([P, width(part)], F32, name="bank")
+            n = [r * P < c.stop for c in W_CHUNKS].index(True)
+            col = r * P - W_CHUNKS[n].start
             for a in range(PASSES):
                 nc.tensor.matmul_mx(
                     out=acc[:],
-                    lhsT=w_sb[c][:, a, col : col + P].bitcast(FP8X4),
+                    lhsT=w_sb[n][:, a, col : col + P].bitcast(FP8X4),
                     lhsT_scale=ws_sb[4 * a : P, r * P : (r + 1) * P],
-                    rhs=xq_sb[a][h][:].bitcast(FP8X4),
-                    rhs_scale=xs_sb[a][h][:],
+                    rhs=xq_sb[a][:, part].bitcast(FP8X4),
+                    rhs_scale=xs_sb[a][:, part],
                     start=(a == 0),
                     stop=(a == PASSES - 1),
                 )
-            y = ypool.tile([P, SH], F32, name="y")
+            y = keep.tile([P, width(part)], F32, name=f"y{r}_{part.start}")
             nc.scalar.activation(y[:], acc[:], SILU, bias=bcol[:, r : r + 1])
             return y
 
-        def scatter(r, h, y):
+        def scatter(r, part, y):
             nc.vector.tensor_tensor(
-                win_sb[r % WINDOWS][:].indirect(offs2_sb[:, h * OH : (h + 1) * OH]), y[:], wgo_sb[h][:], MULT
+                win_sb[r % WINDOWS][:].indirect(offs2_sb[:, columns(part)]), y[:], wgo_sb[:, part], MULT
             )
 
+        def store(r):
+            nc.sync.dma_start(out=out[r * P : (r + 1) * P, :], in_=win_sb[r % WINDOWS][:])
+
         for i in range(PACK):
-            for h in range(HALVES):
-                gather(0, i, h)
-        interleave(0, 0)
-        interleave(0, 1)
-        gather(1, 0, 0)
-        gather(1, 1, 0)
-        quantize(0, 0)
-        gather(1, 2, 0)
-        gather(1, 0, 1)
-        gather(1, 3, 0)
-        gather(1, 1, 1)
-        interleave_shared(1, 0)
-        quantize(0, 1)
-        quantize(1, 0)
-        gather(1, 2, 1)
-        gather(1, 3, 1)
-        for base in range(0, ROW_TILES, WINDOWS):
-            for h in range(HALVES):
-                for r in range(base, base + WINDOWS):
-                    scatter(r, h, multiply(r, h))
-                    if h == HALVES - 1:
-                        nc.sync.dma_start(out=out[r * P : (r + 1) * P, :], in_=win_sb[r % WINDOWS][:])
-                    if (r, h) == (1, 0):
-                        interleave(1, 1)
-                        quantize(1, 1)
+            gather(g0[:, i, :], 0, i, WHOLE)
+        interleave(xb0[:], g0[:])
+        for i in range(PACK):
+            gather(g1_first[:, i, :], 1, i, FIRST)
+            if i < 2:
+                gather(rest_row(i), 1, i, REST)
+        interleave(xb1[0], g1_first[:])
+        quantize(0, WHOLE, xb0[:])
+        gather(rest_row(2), 1, 2, REST)
+        quantize(1, FIRST, xb1[0])
+        gather(rest_row(3), 1, 3, REST)
+        for n, part in enumerate(PIECES):
+            ys = [multiply(r, part) for r in range(STAGED)]
+            if n + 1 < len(PIECES):
+                nxt = PIECES[n + 1]
+                interleave(xb1[n + 1], g1_rest[:, :, nxt.start - REST.start : nxt.stop - REST.start])
+            for r in range(STAGED):
+                scatter(r, part, ys[r])
+                if n + 1 == len(PIECES):
+                    store(r)
+                elif r == 1:
+                    quantize(1, nxt, xb1[n + 1])
+        for r in range(STAGED, ROW_TILES):
+            scatter(r, WHOLE, multiply(r, WHOLE))
+            store(r)

@@ -10,14 +10,16 @@ P = 128
 PACK = 4
 PASSES = K // (P * PACK)
 ROW_TILES = M // P
-WINDOWS = 4
-STAGED = 3
-PIECES = (slice(0, 128), slice(128, 256), slice(256, 512))
-FIRST = PIECES[0]
-REST = slice(128, 512)
+GROUP = 16
+
+FIRST, MIDDLE, LAST = slice(0, 128), slice(128, 256), slice(256, S)
+FRONT = slice(FIRST.start, MIDDLE.stop)
+REST = slice(MIDDLE.start, LAST.stop)
 WHOLE = slice(0, S)
-PITCH = 768
-W_CHUNKS = (slice(0, 256), slice(256, 512), slice(512, 1024))
+
+EARLY = 3
+WINDOWS = EARLY + 1
+W_CHUNKS = (slice(0, 2 * P), slice(2 * P, 4 * P), slice(4 * P, M))
 
 F32 = mybir.dt.float32
 BF16 = mybir.dt.bfloat16
@@ -35,7 +37,7 @@ def width(part):
 
 
 def columns(part):
-    return slice(part.start // 16, part.stop // 16)
+    return slice(part.start // GROUP, part.stop // GROUP)
 
 
 def tile_list_hboth_silu_kernel(tc, xT, w_words, w_scales, wgt, b, wgo, offs, offs2, out):
@@ -44,28 +46,27 @@ def tile_list_hboth_silu_kernel(tc, xT, w_words, w_scales, wgt, b, wgo, offs, of
         keep = ctx.enter_context(tc.tile_pool(name="keep", bufs=1))
         psum = ctx.enter_context(tc.psum_pool(name="psum", bufs=8))
 
-        offs_sb = keep.tile([P, S // 16], U16, name="offs_sb")
-        offs2_sb = keep.tile([P, S // 16], U16, name="offs2_sb")
+        offs_sb = keep.tile([P, S // GROUP], U16, name="offs_sb")
+        offs2_sb = keep.tile([P, S // GROUP], U16, name="offs2_sb")
         wgo_sb = keep.tile([P, S], F32, name="wgo_sb")
         x_sb = [[keep.tile([P, T], F32, name=f"x{a}_{i}") for i in range(PACK)] for a in range(PASSES)]
         g0 = keep.tile([P, PACK, S], F32, name="g0")
-        g1_first = keep.tile([P, PACK, width(FIRST)], F32, name="g1_first")
-        arena = keep.tile([P, PACK * PITCH], F32, name="arena", align_bytes=64)
-        g1_rest = arena[:].rearrange("p (i c) -> p i c", i=PACK)[:, :, 0 : width(REST)]
-        wgt_at = 2 * PITCH + width(REST) - width(FIRST)
-        wgt_sb = arena[:, wgt_at : wgt_at + S]
-        xb1_first = arena[:, 3 * PITCH : 3 * PITCH + 2 * width(FIRST)].bitcast(BF16).rearrange("p (s i) -> p s i", i=PACK)
+        g1_flat = keep.tile([P, PACK * S], F32, name="g1_flat", align_bytes=64)
+        g1 = g1_flat[:].rearrange("p (i s) -> p i s", i=PACK)
+        wgt_sb = keep.tile([P, S], F32, name="wgt_sb")
+        held = 2 * S + REST.start
+        xb1_first = g1_flat[:, held : held + width(FIRST) * PACK // 2].bitcast(BF16).rearrange("p (s i) -> p s i", i=PACK)
         xb0 = keep.tile([P, S, PACK], BF16, name="xb0", align_bytes=64)
-        xb1 = [xb1_first] + [keep.tile([P, width(c), PACK], BF16, name=f"xb1_{c.start}", align_bytes=64)[:] for c in PIECES[1:]]
+        xb1_middle = keep.tile([P, width(MIDDLE), PACK], BF16, name="xb1_middle", align_bytes=64)
+        xb1_last = keep.tile([P, width(LAST), PACK], BF16, name="xb1_last", align_bytes=64)
         xq_sb = [keep.tile([P, S], U32, name=f"xq{a}", align_bytes=64) for a in range(PASSES)]
         xs_sb = [keep.tile([P, S], U8, name=f"xs{a}", align_bytes=64) for a in range(PASSES)]
         w_sb = [keep.tile([P, PASSES, width(c)], I32, name=f"w{n}", align_bytes=64) for n, c in enumerate(W_CHUNKS)]
         ws_sb = keep.tile([P, M], U8, name="ws_sb", align_bytes=64)
-        win_sb = [keep.tile([P, T], F32, name=f"win{r}") for r in range(WINDOWS)]
-        brow = keep.tile([P, P], F32, name="brow")
+        win_sb = [keep.tile([P, T], F32, name=f"win{n}") for n in range(WINDOWS)]
+        b_rows = keep.tile([P, P], F32, name="b_rows")
         ident = keep.tile([P, P], F32, name="ident")
-        bcol = keep.tile([P, ROW_TILES], F32, name="bcol")
-        warm = keep.tile([P, 1], F32, name="warm")
+        b_cols = keep.tile([P, ROW_TILES], F32, name="b_cols")
 
         x_view = xT.rearrange("(a p i) t -> a i p t", p=P, i=PACK)
         w_view = w_words.rearrange("a p n t -> p a (n t)")
@@ -75,7 +76,7 @@ def tile_list_hboth_silu_kernel(tc, xT, w_words, w_scales, wgt, b, wgo, offs, of
             nc.sync.dma_start(out=w_sb[n][:], in_=w_view[:, :, PACK * c.start : PACK * c.stop].bitcast(I32))
 
         nc.sync.dma_start(offs_sb[:], offs)
-        nc.sync.dma_start(out=wgt_sb, in_=wgt)
+        nc.sync.dma_start(out=wgt_sb[:], in_=wgt)
         for a in range(PASSES):
             for i in range(PACK):
                 nc.sync.dma_start(out=x_sb[a][i][:], in_=x_view[a, i])
@@ -86,60 +87,59 @@ def tile_list_hboth_silu_kernel(tc, xT, w_words, w_scales, wgt, b, wgo, offs, of
         nc.sync.dma_start(out=wgo_sb[:, REST], in_=wgo[:, REST])
         load_w(2)
 
-        nc.gpsimd.memset(warm[:], 0.0)
-        nc.scalar.activation(warm[:], warm[:], SILU)
+        for window in win_sb:
+            nc.vector.memset(window[:].bitcast(I32), 0)
+
+        nc.scalar.activation(b_rows[:], win_sb[0][:, 0:P], SILU)
         make_identity(nc, ident[:])
-        nc.gpsimd.memset(brow[:], 0.0)
         nc.gpsimd.memset(ws_sb[:].bitcast(I32), 0)
-        for q in range(4):
+        for q in range(P // 32):
             nc.gpsimd.dma_start(
-                out=ws_sb[32 * q : 32 * q + 8, :].bitcast(I32),
+                out=ws_sb[32 * q : 32 * q + 4 * PASSES, :].bitcast(I32),
                 in_=w_scales[:, 4 * q : 4 * q + 4, :].bitcast(I32),
             )
-        nc.gpsimd.dma_start(out=brow[0:ROW_TILES, :], in_=b.rearrange("(r p) -> r p", p=P))
-
-        for w in range(WINDOWS):
-            nc.vector.memset(win_sb[w][:].bitcast(I32), 0)
+        nc.gpsimd.dma_start(out=b_rows[0:ROW_TILES, :], in_=b.rearrange("(r p) -> r p", p=P))
 
         bank = psum.tile([P, P], F32, name="bank")
-        nc.tensor.transpose(bank[:], brow[:], ident[:])
-        nc.scalar.copy(bcol[:], bank[:, 0:ROW_TILES])
+        nc.tensor.transpose(bank[:], b_rows[:], ident[:])
+        nc.scalar.copy(b_cols[:], bank[:, 0:ROW_TILES])
 
-        def gather(dst, a, i, part):
-            nc.vector.tensor_tensor(dst, x_sb[a][i][:].indirect(offs_sb[:, columns(part)]), wgt_sb[:, part], MULT)
+        def gather(products, a, i, part):
+            nc.vector.tensor_tensor(products, x_sb[a][i][:].indirect(offs_sb[:, columns(part)]), wgt_sb[:, part], MULT)
 
-        def rest_row(i):
-            return arena[:, i * PITCH : i * PITCH + width(REST)]
+        def g1_row(i, part):
+            return g1_flat[:, i * S + part.start : i * S + part.stop]
 
-        def interleave(dst, src):
+        def interleave(rounded, products):
             nc.scalar.copy(
-                dst.rearrange("p (c e) i -> p c i e", e=4),
-                src.rearrange("p i (c e) -> p c i e", e=4),
+                rounded.rearrange("p (c e) i -> p c i e", e=4),
+                products.rearrange("p i (c e) -> p c i e", e=4),
             )
 
-        def quantize(a, part, src):
+        def quantize(a, part, rounded):
             nc.vector.quantize_mx(
                 out=xq_sb[a][:, part].bitcast(FP8X4),
                 scales=xs_sb[a][:, part],
-                in_=src.rearrange("p s i -> p (s i)"),
+                in_=rounded.rearrange("p s i -> p (s i)"),
             )
 
         def multiply(r, part):
             acc = psum.tile([P, width(part)], F32, name="bank")
             n = [r * P < c.stop for c in W_CHUNKS].index(True)
             col = r * P - W_CHUNKS[n].start
-            for a in range(PASSES):
-                nc.tensor.matmul_mx(
-                    out=acc[:],
-                    lhsT=w_sb[n][:, a, col : col + P].bitcast(FP8X4),
-                    lhsT_scale=ws_sb[4 * a : P, r * P : (r + 1) * P],
-                    rhs=xq_sb[a][:, part].bitcast(FP8X4),
-                    rhs_scale=xs_sb[a][:, part],
-                    start=(a == 0),
-                    stop=(a == PASSES - 1),
-                )
+            for piece in (MIDDLE, LAST) if part == REST else (part,):
+                for a in range(PASSES):
+                    nc.tensor.matmul_mx(
+                        out=acc[:, piece.start - part.start : piece.stop - part.start],
+                        lhsT=w_sb[n][:, a, col : col + P].bitcast(FP8X4),
+                        lhsT_scale=ws_sb[4 * a : P, r * P : (r + 1) * P],
+                        rhs=xq_sb[a][:, piece].bitcast(FP8X4),
+                        rhs_scale=xs_sb[a][:, piece],
+                        start=(a == 0),
+                        stop=(a == PASSES - 1),
+                    )
             y = keep.tile([P, width(part)], F32, name=f"y{r}_{part.start}")
-            nc.scalar.activation(y[:], acc[:], SILU, bias=bcol[:, r : r + 1])
+            nc.scalar.activation(y[:], acc[:], SILU, bias=b_cols[:, r : r + 1])
             return y
 
         def scatter(r, part, y):
@@ -147,32 +147,28 @@ def tile_list_hboth_silu_kernel(tc, xT, w_words, w_scales, wgt, b, wgo, offs, of
                 win_sb[r % WINDOWS][:].indirect(offs2_sb[:, columns(part)]), y[:], wgo_sb[:, part], MULT
             )
 
-        def store(r):
-            nc.sync.dma_start(out=out[r * P : (r + 1) * P, :], in_=win_sb[r % WINDOWS][:])
-
         for i in range(PACK):
             gather(g0[:, i, :], 0, i, WHOLE)
         interleave(xb0[:], g0[:])
         for i in range(PACK):
-            gather(g1_first[:, i, :], 1, i, FIRST)
-            if i < 2:
-                gather(rest_row(i), 1, i, REST)
-        interleave(xb1[0], g1_first[:])
+            part = WHOLE if i < 2 else FIRST
+            gather(g1_row(i, part), 1, i, part)
+        interleave(xb1_first, g1[:, :, FIRST])
         quantize(0, WHOLE, xb0[:])
-        gather(rest_row(2), 1, 2, REST)
-        quantize(1, FIRST, xb1[0])
-        gather(rest_row(3), 1, 3, REST)
-        for n, part in enumerate(PIECES):
-            ys = [multiply(r, part) for r in range(STAGED)]
-            if n + 1 < len(PIECES):
-                nxt = PIECES[n + 1]
-                interleave(xb1[n + 1], g1_rest[:, :, nxt.start - REST.start : nxt.stop - REST.start])
-            for r in range(STAGED):
-                scatter(r, part, ys[r])
-                if n + 1 == len(PIECES):
-                    store(r)
-                elif r == 1:
-                    quantize(1, nxt, xb1[n + 1])
-        for r in range(STAGED, ROW_TILES):
-            scatter(r, WHOLE, multiply(r, WHOLE))
-            store(r)
+        gather(g1_row(3, REST), 1, 3, REST)
+        quantize(1, FIRST, xb1_first)
+        gather(g1_row(2, REST), 1, 2, REST)
+
+        ys = [multiply(r, FIRST) for r in range(EARLY)]
+        interleave(xb1_middle[:], g1[:, :, MIDDLE])
+        interleave(xb1_last[:], g1[:, :, LAST])
+        scatter(0, FIRST, ys[0])
+        scatter(1, FIRST, ys[1])
+        quantize(1, MIDDLE, xb1_middle[:])
+        scatter(2, FIRST, ys[2])
+        quantize(1, LAST, xb1_last[:])
+        scatter(EARLY, FRONT, multiply(EARLY, FRONT))
+        for r in range(ROW_TILES):
+            part = REST if r < EARLY else LAST if r == EARLY else WHOLE
+            scatter(r, part, multiply(r, part))
+            nc.sync.dma_start(out=out[r * P : (r + 1) * P, :], in_=win_sb[r % WINDOWS][:])

@@ -10,6 +10,7 @@ P = 128
 PACK = 4
 PASSES = K // (P * PACK)
 ROW_TILES = M // P
+BLOCK = 32
 GROUP = 16
 
 FIRST, MIDDLE, LAST = slice(0, 128), slice(128, 256), slice(256, S)
@@ -18,7 +19,7 @@ REST = slice(MIDDLE.start, LAST.stop)
 WHOLE = slice(0, S)
 
 EARLY = 3
-WINDOWS = EARLY + 1
+WINDOWS = EARLY
 W_CHUNKS = (slice(0, 2 * P), slice(2 * P, 4 * P), slice(4 * P, M))
 
 F32 = mybir.dt.float32
@@ -53,7 +54,10 @@ def tile_list_hboth_silu_kernel(tc, xT, w_words, w_scales, wgt, b, wgo, offs, of
         g0 = keep.tile([P, PACK, S], F32, name="g0")
         g1_flat = keep.tile([P, PACK * S], F32, name="g1_flat", align_bytes=64)
         g1 = g1_flat[:].rearrange("p (i s) -> p i s", i=PACK)
-        wgt_sb = keep.tile([P, S], F32, name="wgt_sb")
+        wgt_dealt = keep.tile([P, BLOCK], F32, name="wgt_dealt", align_bytes=64)
+        wgt_turned = keep.tile([P, BLOCK], F32, name="wgt_turned", align_bytes=64)
+        wgt_spread = keep.tile([P, S], F32, name="wgt_spread", align_bytes=64)
+        wgt_sb = keep.tile([P, S], F32, name="wgt_sb", align_bytes=64)
         held = 2 * S + REST.start
         xb1_first = g1_flat[:, held : held + width(FIRST) * PACK // 2].bitcast(BF16).rearrange("p (s i) -> p s i", i=PACK)
         xb0 = keep.tile([P, S, PACK], BF16, name="xb0", align_bytes=64)
@@ -75,8 +79,8 @@ def tile_list_hboth_silu_kernel(tc, xT, w_words, w_scales, wgt, b, wgo, offs, of
             c = W_CHUNKS[n]
             nc.sync.dma_start(out=w_sb[n][:], in_=w_view[:, :, PACK * c.start : PACK * c.stop].bitcast(I32))
 
+        nc.sync.dma_start(out=wgt_dealt[:], in_=wgt.rearrange("(g q) (r c) -> g q r c", q=GROUP, c=BLOCK)[:, 0])
         nc.sync.dma_start(offs_sb[:], offs)
-        nc.sync.dma_start(out=wgt_sb[:], in_=wgt)
         for a in range(PASSES):
             for i in range(PACK):
                 nc.sync.dma_start(out=x_sb[a][i][:], in_=x_view[a, i])
@@ -89,6 +93,16 @@ def tile_list_hboth_silu_kernel(tc, xT, w_words, w_scales, wgt, b, wgo, offs, of
 
         for window in win_sb:
             nc.vector.memset(window[:].bitcast(I32), 0)
+
+        nc.vector.transpose(wgt_turned[:], wgt_dealt[:])
+        spread = wgt_spread[:].rearrange("p (r h q) -> p r h q", h=BLOCK // GROUP, q=GROUP)
+        turned = wgt_turned[:].rearrange("p (h r) -> p r h", r=GROUP)
+        for rows in (slice(0, GROUP // 2), slice(GROUP // 2, GROUP)):
+            nc.vector.tensor_copy(
+                spread[:, rows], turned[:, rows].unsqueeze(3).to_broadcast([P, GROUP // 2, BLOCK // GROUP, GROUP])
+            )
+        for part in (FRONT, LAST):
+            nc.vector.transpose(wgt_sb[:, part], wgt_spread[:, part])
 
         nc.scalar.activation(b_rows[:], win_sb[0][:, 0:P], SILU)
         make_identity(nc, ident[:])
@@ -115,6 +129,10 @@ def tile_list_hboth_silu_kernel(tc, xT, w_words, w_scales, wgt, b, wgo, offs, of
                 rounded.rearrange("p (c e) i -> p c i e", e=4),
                 products.rearrange("p i (c e) -> p c i e", e=4),
             )
+
+        def interleave_pair(rounded, products, pair):
+            planes = slice(2 * pair, 2 * pair + 2)
+            interleave(rounded[:, :, planes], products[:, planes, :])
 
         def quantize(a, part, rounded):
             nc.vector.quantize_mx(
@@ -148,11 +166,14 @@ def tile_list_hboth_silu_kernel(tc, xT, w_words, w_scales, wgt, b, wgo, offs, of
             )
 
         for i in range(PACK):
-            gather(g0[:, i, :], 0, i, WHOLE)
+            for part in (FRONT, LAST) if i == 0 else (WHOLE,):
+                gather(g0[:, i, part], 0, i, part)
         interleave(xb0[:], g0[:])
         for i in range(PACK):
             part = WHOLE if i < 2 else FIRST
             gather(g1_row(i, part), 1, i, part)
+            if i == 1:
+                interleave_pair(xb1_last[:], g1[:, :, LAST], 0)
         interleave(xb1_first, g1[:, :, FIRST])
         quantize(0, WHOLE, xb0[:])
         gather(g1_row(3, REST), 1, 3, REST)
@@ -161,14 +182,15 @@ def tile_list_hboth_silu_kernel(tc, xT, w_words, w_scales, wgt, b, wgo, offs, of
 
         ys = [multiply(r, FIRST) for r in range(EARLY)]
         interleave(xb1_middle[:], g1[:, :, MIDDLE])
-        interleave(xb1_last[:], g1[:, :, LAST])
+        interleave_pair(xb1_last[:], g1[:, :, LAST], 1)
         scatter(0, FIRST, ys[0])
         scatter(1, FIRST, ys[1])
         quantize(1, MIDDLE, xb1_middle[:])
         scatter(2, FIRST, ys[2])
         quantize(1, LAST, xb1_last[:])
-        scatter(EARLY, FRONT, multiply(EARLY, FRONT))
+        for r in range(EARLY - 1):
+            scatter(r, MIDDLE, multiply(r, MIDDLE))
         for r in range(ROW_TILES):
-            part = REST if r < EARLY else LAST if r == EARLY else WHOLE
+            part = LAST if r < EARLY - 1 else REST if r < EARLY else WHOLE
             scatter(r, part, multiply(r, part))
             nc.sync.dma_start(out=out[r * P : (r + 1) * P, :], in_=win_sb[r % WINDOWS][:])

@@ -66,9 +66,7 @@ def tile_list_hboth_silu_kernel(tc, xT, w_words, w_scales, wgt, b, wgo, offs, of
         xq_sb = [keep.tile([P, S], U32, name=f"xq{a}", align_bytes=64) for a in range(PASSES)]
         xs_sb = [keep.tile([P, S], U8, name=f"xs{a}", align_bytes=64) for a in range(PASSES)]
         w_sb = [keep.tile([P, PASSES, width(c)], I32, name=f"w{n}", align_bytes=64) for n, c in enumerate(W_CHUNKS)]
-        ws_sb = keep.tile([P, M], U8, name="ws_sb", align_bytes=64)
         win_sb = [keep.tile([P, T], F32, name=f"win{n}") for n in range(WINDOWS)]
-        b_rows = keep.tile([P, P], F32, name="b_rows")
         ident = keep.tile([P, P], F32, name="ident")
         b_cols = keep.tile([P, ROW_TILES], F32, name="b_cols")
 
@@ -104,6 +102,8 @@ def tile_list_hboth_silu_kernel(tc, xT, w_words, w_scales, wgt, b, wgo, offs, of
         for part in (FRONT, LAST):
             nc.vector.transpose(wgt_sb[:, part], wgt_spread[:, part])
 
+        ws_sb = keep.tile([P, M], U8, name="ws_sb", tag="wgt_spread", align_bytes=64)
+        b_rows = keep.tile([P, P], F32, name="b_rows", tag="wgt_turned", align_bytes=64)
         nc.scalar.activation(b_rows[:], win_sb[0][:, 0:P], SILU)
         make_identity(nc, ident[:])
         nc.gpsimd.memset(ws_sb[:].bitcast(I32), 0)

@@ -64,7 +64,8 @@ def tile_list_hboth_silu_kernel(tc, xT, w_words, w_scales, wgt, b, wgo, offs, of
         xb1_middle = keep.tile([P, width(MIDDLE), PACK], BF16, name="xb1_middle", align_bytes=64)
         xb1_last = keep.tile([P, width(LAST), PACK], BF16, name="xb1_last", align_bytes=64)
         xq_sb = [keep.tile([P, S], U32, name=f"xq{a}", align_bytes=64) for a in range(PASSES)]
-        xs_sb = [keep.tile([P, S], U8, name=f"xs{a}", align_bytes=64) for a in range(PASSES)]
+        xs_both = keep.tile([P, S + width(FRONT)], U8, name="xs_both", align_bytes=64)
+        xs_sb = [xs_both[4:P, 0:S], xs_both[:, width(FRONT) : width(FRONT) + S]]
         w_sb = [keep.tile([P, PASSES, width(c)], I32, name=f"w{n}", align_bytes=64) for n, c in enumerate(W_CHUNKS)]
         win_sb = [keep.tile([P, T], F32, name=f"win{n}") for n in range(WINDOWS)]
         ident = keep.tile([P, P], F32, name="ident")
@@ -175,12 +176,14 @@ def tile_list_hboth_silu_kernel(tc, xT, w_words, w_scales, wgt, b, wgo, offs, of
             if i == 1:
                 interleave_pair(xb1_last[:], g1[:, :, LAST], 0)
         interleave(xb1_first, g1[:, :, FIRST])
-        quantize(0, WHOLE, xb0[:])
+        quantize(0, FRONT, xb0[:, FRONT, :])
         gather(g1_row(3, REST), 1, 3, REST)
         quantize(1, FIRST, xb1_first)
         gather(g1_row(2, REST), 1, 2, REST)
 
-        ys = [multiply(r, FIRST) for r in range(EARLY)]
+        ys = [multiply(r, FIRST) for r in range(2)]
+        quantize(0, LAST, xb0[:, LAST, :])
+        ys.extend(multiply(r, FIRST) for r in range(2, EARLY))
         interleave(xb1_middle[:], g1[:, :, MIDDLE])
         interleave_pair(xb1_last[:], g1[:, :, LAST], 1)
         scatter(0, FIRST, ys[0])

@@ -10,7 +10,8 @@ P = 128
 PACK = 4
 PASSES = K // (P * PACK)
 ROW_TILES = M // P
-BLOCK = 32
+SQUARE = 32
+SCALE_ROWS = 4
 GROUP = 16
 
 FIRST, MIDDLE, LAST = slice(0, 128), slice(128, 256), slice(256, S)
@@ -20,7 +21,8 @@ WHOLE = slice(0, S)
 
 EARLY = 3
 WINDOWS = EARLY
-W_CHUNKS = (slice(0, 2 * P), slice(2 * P, 4 * P), slice(4 * P, M))
+FIRST_CHUNK_TILES = 2
+W_CHUNKS = (slice(0, FIRST_CHUNK_TILES * P), slice(FIRST_CHUNK_TILES * P, 4 * P), slice(4 * P, M))
 
 F32 = mybir.dt.float32
 BF16 = mybir.dt.bfloat16
@@ -54,20 +56,21 @@ def tile_list_hboth_silu_kernel(tc, xT, w_words, w_scales, wgt, b, wgo, offs, of
         g0 = keep.tile([P, PACK, S], F32, name="g0")
         g1_flat = keep.tile([P, PACK * S], F32, name="g1_flat", align_bytes=64)
         g1 = g1_flat[:].rearrange("p (i s) -> p i s", i=PACK)
-        wgt_dealt = keep.tile([P, BLOCK], F32, name="wgt_dealt", align_bytes=64)
-        wgt_turned = keep.tile([P, BLOCK], F32, name="wgt_turned", align_bytes=64)
+        wgt_dealt = keep.tile([P, SQUARE], F32, name="wgt_dealt", align_bytes=64)
+        wgt_turned = keep.tile([P, SQUARE], F32, name="wgt_turned", align_bytes=64)
         wgt_spread = keep.tile([P, S], F32, name="wgt_spread", align_bytes=64)
         wgt_sb = keep.tile([P, S], F32, name="wgt_sb", align_bytes=64)
         held = 2 * S + REST.start
-        xb1_first = g1_flat[:, held : held + width(FIRST) * PACK // 2].bitcast(BF16).rearrange("p (s i) -> p s i", i=PACK)
+        xb1_first = g1_flat[:, held : held + width(FIRST) * PACK // 2].bitcast(BF16)
+        xb1_first = xb1_first.rearrange("p (s i) -> p s i", i=PACK)
         xb0 = keep.tile([P, S, PACK], BF16, name="xb0", align_bytes=64)
         xb1_middle = keep.tile([P, width(MIDDLE), PACK], BF16, name="xb1_middle", align_bytes=64)
         xb1_last = keep.tile([P, width(LAST), PACK], BF16, name="xb1_last", align_bytes=64)
         xq_sb = [keep.tile([P, S], U32, name=f"xq{a}", align_bytes=64) for a in range(PASSES)]
         xs_both = keep.tile([P, S + width(FRONT)], U8, name="xs_both", align_bytes=64)
-        xs_sb = [xs_both[4:P, 0:S], xs_both[:, width(FRONT) : width(FRONT) + S]]
+        xs_sb = [xs_both[SCALE_ROWS:P, 0:S], xs_both[:, width(FRONT) : width(FRONT) + S]]
         w_sb = [keep.tile([P, PASSES, width(c)], I32, name=f"w{n}", align_bytes=64) for n, c in enumerate(W_CHUNKS)]
-        win_sb = [keep.tile([P, T], F32, name=f"win{n}") for n in range(WINDOWS)]
+        win_sb = [keep.tile([P, T], F32, name=f"win{n}") for n in range(WINDOWS - 1)]
         ident = keep.tile([P, P], F32, name="ident")
         b_cols = keep.tile([P, ROW_TILES], F32, name="b_cols")
 
@@ -78,7 +81,7 @@ def tile_list_hboth_silu_kernel(tc, xT, w_words, w_scales, wgt, b, wgo, offs, of
             c = W_CHUNKS[n]
             nc.sync.dma_start(out=w_sb[n][:], in_=w_view[:, :, PACK * c.start : PACK * c.stop].bitcast(I32))
 
-        nc.sync.dma_start(out=wgt_dealt[:], in_=wgt.rearrange("(g q) (r c) -> g q r c", q=GROUP, c=BLOCK)[:, 0])
+        nc.sync.dma_start(out=wgt_dealt[:], in_=wgt.rearrange("(g q) (r c) -> g q r c", q=GROUP, c=SQUARE)[:, 0])
         nc.sync.dma_start(offs_sb[:], offs)
         for a in range(PASSES):
             for i in range(PACK):
@@ -94,11 +97,11 @@ def tile_list_hboth_silu_kernel(tc, xT, w_words, w_scales, wgt, b, wgo, offs, of
             nc.vector.memset(window[:].bitcast(I32), 0)
 
         nc.vector.transpose(wgt_turned[:], wgt_dealt[:])
-        spread = wgt_spread[:].rearrange("p (r h q) -> p r h q", h=BLOCK // GROUP, q=GROUP)
+        spread = wgt_spread[:].rearrange("p (r h q) -> p r h q", h=SQUARE // GROUP, q=GROUP)
         turned = wgt_turned[:].rearrange("p (h r) -> p r h", r=GROUP)
         for rows in (slice(0, GROUP // 2), slice(GROUP // 2, GROUP)):
             nc.vector.tensor_copy(
-                spread[:, rows], turned[:, rows].unsqueeze(3).to_broadcast([P, GROUP // 2, BLOCK // GROUP, GROUP])
+                spread[:, rows], turned[:, rows].unsqueeze(3).to_broadcast([P, GROUP // 2, SQUARE // GROUP, GROUP])
             )
         for part in (FRONT, LAST):
             nc.vector.transpose(wgt_sb[:, part], wgt_spread[:, part])
@@ -108,10 +111,10 @@ def tile_list_hboth_silu_kernel(tc, xT, w_words, w_scales, wgt, b, wgo, offs, of
         nc.scalar.activation(b_rows[:], win_sb[0][:, 0:P], SILU)
         make_identity(nc, ident[:])
         nc.gpsimd.memset(ws_sb[:].bitcast(I32), 0)
-        for q in range(P // 32):
+        for q in range(P // SQUARE):
             nc.gpsimd.dma_start(
-                out=ws_sb[32 * q : 32 * q + 4 * PASSES, :].bitcast(I32),
-                in_=w_scales[:, 4 * q : 4 * q + 4, :].bitcast(I32),
+                out=ws_sb[SQUARE * q : SQUARE * q + SCALE_ROWS * PASSES, :].bitcast(I32),
+                in_=w_scales[:, SCALE_ROWS * q : SCALE_ROWS * (q + 1), :].bitcast(I32),
             )
         nc.gpsimd.dma_start(out=b_rows[0:ROW_TILES, :], in_=b.rearrange("(r p) -> r p", p=P))
 
@@ -151,7 +154,7 @@ def tile_list_hboth_silu_kernel(tc, xT, w_words, w_scales, wgt, b, wgo, offs, of
                     nc.tensor.matmul_mx(
                         out=acc[:, piece.start - part.start : piece.stop - part.start],
                         lhsT=w_sb[n][:, a, col : col + P].bitcast(FP8X4),
-                        lhsT_scale=ws_sb[4 * a : P, r * P : (r + 1) * P],
+                        lhsT_scale=ws_sb[SCALE_ROWS * a : P, r * P : (r + 1) * P],
                         rhs=xq_sb[a][:, piece].bitcast(FP8X4),
                         rhs_scale=xs_sb[a][:, piece],
                         start=(a == 0),
@@ -170,10 +173,12 @@ def tile_list_hboth_silu_kernel(tc, xT, w_words, w_scales, wgt, b, wgo, offs, of
             for part in (FRONT, LAST) if i == 0 else (WHOLE,):
                 gather(g0[:, i, part], 0, i, part)
         interleave(xb0[:], g0[:])
+        win_sb.append(keep.tile([P, T], F32, name="win_last", tag="x0_0"))
+        nc.gpsimd.memset(win_sb[-1][:].bitcast(I32), 0)
         for i in range(PACK):
-            part = WHOLE if i < 2 else FIRST
+            part = WHOLE if i < PACK // 2 else FIRST
             gather(g1_row(i, part), 1, i, part)
-            if i == 1:
+            if i == PACK // 2 - 1:
                 interleave_pair(xb1_last[:], g1[:, :, LAST], 0)
         interleave(xb1_first, g1[:, :, FIRST])
         quantize(0, FRONT, xb0[:, FRONT, :])
@@ -181,9 +186,9 @@ def tile_list_hboth_silu_kernel(tc, xT, w_words, w_scales, wgt, b, wgo, offs, of
         quantize(1, FIRST, xb1_first)
         gather(g1_row(2, REST), 1, 2, REST)
 
-        ys = [multiply(r, FIRST) for r in range(2)]
+        ys = [multiply(r, FIRST) for r in range(FIRST_CHUNK_TILES)]
         quantize(0, LAST, xb0[:, LAST, :])
-        ys.extend(multiply(r, FIRST) for r in range(2, EARLY))
+        ys.extend(multiply(r, FIRST) for r in range(FIRST_CHUNK_TILES, EARLY))
         interleave(xb1_middle[:], g1[:, :, MIDDLE])
         interleave_pair(xb1_last[:], g1[:, :, LAST], 1)
         scatter(0, FIRST, ys[0])

@@ -81,17 +81,13 @@ def tile_list_hboth_silu_kernel(tc, xT, w_words, w_scales, wgt, b, wgo, offs, of
             c = W_CHUNKS[n]
             nc.sync.dma_start(out=w_sb[n][:], in_=w_view[:, :, PACK * c.start : PACK * c.stop].bitcast(I32))
 
-        nc.sync.dma_start(out=wgt_dealt[:], in_=wgt.rearrange("(g q) (r c) -> g q r c", q=GROUP, c=SQUARE)[:, 0])
+        nc.scalar.dma_start(out=wgt_dealt[:], in_=wgt.rearrange("(g q) (r c) -> g q r c", q=GROUP, c=SQUARE)[:, 0])
+        b_rows = keep.tile([P, P], F32, name="b_rows", align_bytes=64)
+        nc.scalar.dma_start(out=b_rows[P - ROW_TILES : P, :], in_=b.rearrange("(r p) -> r p", p=P))
         nc.sync.dma_start(offs_sb[:], offs)
         for a in range(PASSES):
             for i in range(PACK):
                 nc.sync.dma_start(out=x_sb[a][i][:], in_=x_view[a, i])
-        load_w(0)
-        nc.sync.dma_start(offs2_sb[:], offs2)
-        nc.sync.dma_start(out=wgo_sb[:, FIRST], in_=wgo[:, FIRST])
-        load_w(1)
-        nc.sync.dma_start(out=wgo_sb[:, REST], in_=wgo[:, REST])
-        load_w(2)
 
         for window in win_sb:
             nc.vector.memset(window[:].bitcast(I32), 0)
@@ -106,21 +102,35 @@ def tile_list_hboth_silu_kernel(tc, xT, w_words, w_scales, wgt, b, wgo, offs, of
         for part in (FRONT, LAST):
             nc.vector.transpose(wgt_sb[:, part], wgt_spread[:, part])
 
-        ws_sb = keep.tile([P, M], U8, name="ws_sb", tag="wgt_spread", align_bytes=64)
-        b_rows = keep.tile([P, P], F32, name="b_rows", tag="wgt_turned", align_bytes=64)
-        nc.scalar.activation(b_rows[:], win_sb[0][:, 0:P], SILU)
+        ws_sb = [keep.tile([P, M // 2], U8, name=f"ws{h}", align_bytes=64) for h in range(2)]
+        nc.scalar.activation(b_rows[0 : P - ROW_TILES, :], win_sb[0][0 : P - ROW_TILES, 0:P], SILU)
         make_identity(nc, ident[:])
-        nc.gpsimd.memset(ws_sb[:].bitcast(I32), 0)
-        for q in range(P // SQUARE):
-            nc.gpsimd.dma_start(
-                out=ws_sb[SQUARE * q : SQUARE * q + SCALE_ROWS * PASSES, :].bitcast(I32),
-                in_=w_scales[:, SCALE_ROWS * q : SCALE_ROWS * (q + 1), :].bitcast(I32),
-            )
-        nc.gpsimd.dma_start(out=b_rows[0:ROW_TILES, :], in_=b.rearrange("(r p) -> r p", p=P))
+        def load_scales(h):
+            cols = slice(h * M // 2, (h + 1) * M // 2)
+            for q in range(P // SQUARE):
+                nc.sync.dma_start(
+                    out=ws_sb[h][SQUARE * q : SQUARE * q + SCALE_ROWS * PASSES, :].bitcast(I32),
+                    in_=w_scales[:, SCALE_ROWS * q : SCALE_ROWS * (q + 1), cols].bitcast(I32),
+                )
+
+        load_w(0)
+        load_scales(0)
+        nc.sync.dma_start(out=wgo_sb[:, FIRST], in_=wgo[:, FIRST])
+        nc.sync.dma_start(offs2_sb[:], offs2)
+        load_w(1)
+        nc.sync.dma_start(out=wgo_sb[:, REST], in_=wgo[:, REST])
+        load_scales(1)
+        load_w(2)
 
         bank = psum.tile([P, P], F32, name="bank")
         nc.tensor.transpose(bank[:], b_rows[:], ident[:])
-        nc.scalar.copy(b_cols[:], bank[:, 0:ROW_TILES])
+        nc.scalar.copy(b_cols[:], bank[:, P - ROW_TILES : P])
+        b_held = [
+            xb1_middle[:].rearrange("p s i -> p (s i)").bitcast(F32)[:, 0:1],
+            xb1_last[:].rearrange("p s i -> p (s i)").bitcast(F32)[:, 1:2],
+        ]
+        for r in range(FIRST_CHUNK_TILES):
+            nc.scalar.copy(b_held[r], bank[:, P - ROW_TILES + r : P - ROW_TILES + r + 1])
 
         def gather(products, a, i, part):
             nc.vector.tensor_tensor(products, x_sb[a][i][:].indirect(offs_sb[:, columns(part)]), wgt_sb[:, part], MULT)
@@ -154,14 +164,14 @@ def tile_list_hboth_silu_kernel(tc, xT, w_words, w_scales, wgt, b, wgo, offs, of
                     nc.tensor.matmul_mx(
                         out=acc[:, piece.start - part.start : piece.stop - part.start],
                         lhsT=w_sb[n][:, a, col : col + P].bitcast(FP8X4),
-                        lhsT_scale=ws_sb[SCALE_ROWS * a : P, r * P : (r + 1) * P],
+                        lhsT_scale=ws_sb[r // 4][SCALE_ROWS * a : P, r % 4 * P : (r % 4 + 1) * P],
                         rhs=xq_sb[a][:, piece].bitcast(FP8X4),
                         rhs_scale=xs_sb[a][:, piece],
                         start=(a == 0),
                         stop=(a == PASSES - 1),
                     )
             y = keep.tile([P, width(part)], F32, name=f"y{r}_{part.start}")
-            nc.scalar.activation(y[:], acc[:], SILU, bias=b_cols[:, r : r + 1])
+            nc.scalar.activation(y[:], acc[:], SILU, bias=b_held[r] if part == FIRST and r < FIRST_CHUNK_TILES else b_cols[:, r : r + 1])
             return y
 
         def scatter(r, part, y):

@@ -18,6 +18,7 @@ FIRST, MIDDLE, LAST = slice(0, 128), slice(128, 256), slice(256, S)
 FRONT = slice(FIRST.start, MIDDLE.stop)
 REST = slice(MIDDLE.start, LAST.stop)
 WHOLE = slice(0, S)
+PIECES = (FIRST, MIDDLE, LAST)
 
 EARLY = 3
 WINDOWS = EARLY
@@ -60,15 +61,9 @@ def tile_list_hboth_silu_kernel(tc, xT, w_words, w_scales, wgt, b, wgo, offs, of
         wgt_turned = keep.tile([P, SQUARE], F32, name="wgt_turned", align_bytes=64)
         wgt_spread = keep.tile([P, S], F32, name="wgt_spread", align_bytes=64)
         wgt_sb = keep.tile([P, S], F32, name="wgt_sb", align_bytes=64)
-        held = 2 * S + REST.start
-        xb1_first = g1_flat[:, held : held + width(FIRST) * PACK // 2].bitcast(BF16)
-        xb1_first = xb1_first.rearrange("p (s i) -> p s i", i=PACK)
-        xb0 = keep.tile([P, S, PACK], BF16, name="xb0", align_bytes=64)
-        xb1_middle = keep.tile([P, width(MIDDLE), PACK], BF16, name="xb1_middle", align_bytes=64)
-        xb1_last = keep.tile([P, width(LAST), PACK], BF16, name="xb1_last", align_bytes=64)
-        xq_sb = [keep.tile([P, S], U32, name=f"xq{a}", align_bytes=64) for a in range(PASSES)]
-        xs_both = keep.tile([P, S + width(FRONT)], U8, name="xs_both", align_bytes=64)
-        xs_sb = [xs_both[SCALE_ROWS:P, 0:S], xs_both[:, width(FRONT) : width(FRONT) + S]]
+        xb = {c.start: keep.tile([P, PASSES, width(c), PACK], BF16, name=f"xb{c.start}", align_bytes=64) for c in PIECES}
+        xq = {c.start: keep.tile([P, PASSES, width(c)], U32, name=f"xq{c.start}", align_bytes=64) for c in PIECES}
+        xs = {c.start: keep.tile([P, PASSES, width(c)], U8, name=f"xs{c.start}", align_bytes=64) for c in PIECES}
         w_sb = [keep.tile([P, PASSES, width(c)], I32, name=f"w{n}", align_bytes=64) for n, c in enumerate(W_CHUNKS)]
         win_sb = [keep.tile([P, T], F32, name=f"win{n}") for n in range(WINDOWS - 1)]
         ident = keep.tile([P, P], F32, name="ident")
@@ -125,12 +120,8 @@ def tile_list_hboth_silu_kernel(tc, xT, w_words, w_scales, wgt, b, wgo, offs, of
         bank = psum.tile([P, P], F32, name="bank")
         nc.tensor.transpose(bank[:], b_rows[:], ident[:])
         nc.scalar.copy(b_cols[:], bank[:, P - ROW_TILES : P])
-        b_held = [
-            xb1_middle[:].rearrange("p s i -> p (s i)").bitcast(F32)[:, 0:1],
-            xb1_last[:].rearrange("p s i -> p (s i)").bitcast(F32)[:, 1:2],
-        ]
-        for r in range(FIRST_CHUNK_TILES):
-            nc.scalar.copy(b_held[r], bank[:, P - ROW_TILES + r : P - ROW_TILES + r + 1])
+        b_held = xb[LAST.start][:, 1].rearrange("p s i -> p (s i)").bitcast(F32)[:, 1:2]
+        nc.scalar.copy(b_held, bank[:, P - ROW_TILES + 1 : P - ROW_TILES + 2])
 
         def gather(products, a, i, part):
             nc.vector.tensor_tensor(products, x_sb[a][i][:].indirect(offs_sb[:, columns(part)]), wgt_sb[:, part], MULT)
@@ -138,40 +129,34 @@ def tile_list_hboth_silu_kernel(tc, xT, w_words, w_scales, wgt, b, wgo, offs, of
         def g1_row(i, part):
             return g1_flat[:, i * S + part.start : i * S + part.stop]
 
-        def interleave(rounded, products):
-            nc.scalar.copy(
-                rounded.rearrange("p (c e) i -> p c i e", e=4),
-                products.rearrange("p i (c e) -> p c i e", e=4),
-            )
+        def interleave(copy, rounded, products):
+            copy(rounded.rearrange("p (c e) i -> p c i e", e=4), products.rearrange("p i (c e) -> p c i e", e=4))
 
-        def interleave_pair(rounded, products, pair):
-            planes = slice(2 * pair, 2 * pair + 2)
-            interleave(rounded[:, :, planes], products[:, planes, :])
-
-        def quantize(a, part, rounded):
+        def quantize(piece):
             nc.vector.quantize_mx(
-                out=xq_sb[a][:, part].bitcast(FP8X4),
-                scales=xs_sb[a][:, part],
-                in_=rounded.rearrange("p s i -> p (s i)"),
+                out=xq[piece.start][:].rearrange("p a s -> p (a s)").bitcast(FP8X4),
+                scales=xs[piece.start][:].rearrange("p a s -> p (a s)"),
+                in_=xb[piece.start][:].rearrange("p a s i -> p (a s i)"),
             )
 
         def multiply(r, part):
             acc = psum.tile([P, width(part)], F32, name="bank")
             n = [r * P < c.stop for c in W_CHUNKS].index(True)
             col = r * P - W_CHUNKS[n].start
-            for piece in (MIDDLE, LAST) if part == REST else (part,):
-                for a in range(PASSES):
-                    nc.tensor.matmul_mx(
-                        out=acc[:, piece.start - part.start : piece.stop - part.start],
-                        lhsT=w_sb[n][:, a, col : col + P].bitcast(FP8X4),
-                        lhsT_scale=ws_sb[r // 4][SCALE_ROWS * a : P, r % 4 * P : (r % 4 + 1) * P],
-                        rhs=xq_sb[a][:, piece].bitcast(FP8X4),
-                        rhs_scale=xs_sb[a][:, piece],
-                        start=(a == 0),
-                        stop=(a == PASSES - 1),
-                    )
+            for piece in PIECES:
+                if part.start <= piece.start < part.stop:
+                    for a in range(PASSES):
+                        nc.tensor.matmul_mx(
+                            out=acc[:, piece.start - part.start : piece.stop - part.start],
+                            lhsT=w_sb[n][:, a, col : col + P].bitcast(FP8X4),
+                            lhsT_scale=ws_sb[r // 4][SCALE_ROWS * a : P, r % 4 * P : (r % 4 + 1) * P],
+                            rhs=xq[piece.start][:, a].bitcast(FP8X4),
+                            rhs_scale=xs[piece.start][:, a],
+                            start=(a == 0),
+                            stop=(a == PASSES - 1),
+                        )
             y = keep.tile([P, width(part)], F32, name=f"y{r}_{part.start}")
-            nc.scalar.activation(y[:], acc[:], SILU, bias=b_held[r] if part == FIRST and r < FIRST_CHUNK_TILES else b_cols[:, r : r + 1])
+            nc.scalar.activation(y[:], acc[:], SILU, bias=b_held if (r, part) == (1, FIRST) else b_cols[:, r : r + 1])
             return y
 
         def scatter(r, part, y):
@@ -179,36 +164,41 @@ def tile_list_hboth_silu_kernel(tc, xT, w_words, w_scales, wgt, b, wgo, offs, of
                 win_sb[r % WINDOWS][:].indirect(offs2_sb[:, columns(part)]), y[:], wgo_sb[:, part], MULT
             )
 
+        def store(r):
+            nc.sync.dma_start(out=out[r * P : (r + 1) * P, :], in_=win_sb[r % WINDOWS][:])
+
+        low, high = slice(0, 2), slice(2, 4)
         for i in range(PACK):
             for part in (FRONT, LAST) if i == 0 else (WHOLE,):
                 gather(g0[:, i, part], 0, i, part)
-        interleave(xb0[:], g0[:])
+        for piece in PIECES:
+            interleave(nc.scalar.copy, xb[piece.start][:, 0], g0[:, :, piece])
         win_sb.append(keep.tile([P, T], F32, name="win_last", tag="x0_0"))
         nc.gpsimd.memset(win_sb[-1][:].bitcast(I32), 0)
-        for i in range(PACK):
-            part = WHOLE if i < PACK // 2 else FIRST
-            gather(g1_row(i, part), 1, i, part)
-            if i == PACK // 2 - 1:
-                interleave_pair(xb1_last[:], g1[:, :, LAST], 0)
-        interleave(xb1_first, g1[:, :, FIRST])
-        quantize(0, FRONT, xb0[:, FRONT, :])
-        gather(g1_row(3, REST), 1, 3, REST)
-        quantize(1, FIRST, xb1_first)
-        gather(g1_row(2, REST), 1, 2, REST)
-
-        ys = [multiply(r, FIRST) for r in range(FIRST_CHUNK_TILES)]
-        quantize(0, LAST, xb0[:, LAST, :])
-        ys.extend(multiply(r, FIRST) for r in range(FIRST_CHUNK_TILES, EARLY))
-        interleave(xb1_middle[:], g1[:, :, MIDDLE])
-        interleave_pair(xb1_last[:], g1[:, :, LAST], 1)
+        for i in range(2):
+            gather(g1_row(i, WHOLE), 1, i, WHOLE)
+        for piece in (FIRST, LAST):
+            interleave(nc.scalar.copy, xb[piece.start][:, 1, :, low], g1[:, low, piece])
+        gather(g1_row(2, FRONT), 1, 2, FRONT)
+        gather(g1_row(3, FIRST), 1, 3, FIRST)
+        gather(g1_row(3, MIDDLE), 1, 3, MIDDLE)
+        interleave(nc.vector.tensor_copy, xb[FIRST.start][:, 1, :, high], g1[:, high, FIRST])
+        third, fourth = slice(256, 384), slice(384, 512)
+        gather(g1_row(3, third), 1, 3, third)
+        quantize(FIRST)
+        interleave(nc.scalar.copy, xb[MIDDLE.start][:, 1], g1[:, :, MIDDLE])
+        gather(g1_row(3, fourth), 1, 3, fourth)
+        held = 3 * S + width(FIRST) - width(LAST)
+        gather(g1_flat[:, held : held + width(LAST)], 1, 2, LAST)
+        last_pair = g1_flat[:, PACK * S - 2 * width(REST) : PACK * S].rearrange("p (i s) -> p i s", i=2)
+        quantize(MIDDLE)
+        ys = [multiply(r, FIRST) for r in range(2)]
+        interleave(nc.scalar.copy, xb[LAST.start][:, 1, :, high], last_pair[:, :, width(FIRST) : width(REST)])
         scatter(0, FIRST, ys[0])
         scatter(1, FIRST, ys[1])
-        quantize(1, MIDDLE, xb1_middle[:])
-        scatter(2, FIRST, ys[2])
-        quantize(1, LAST, xb1_last[:])
-        for r in range(EARLY - 1):
-            scatter(r, MIDDLE, multiply(r, MIDDLE))
+        quantize(LAST)
+        scatter(2, FRONT, multiply(2, FRONT))
         for r in range(ROW_TILES):
-            part = LAST if r < EARLY - 1 else REST if r < EARLY else WHOLE
+            part = REST if r < 2 else LAST if r == 2 else WHOLE
             scatter(r, part, multiply(r, part))
-            nc.sync.dma_start(out=out[r * P : (r + 1) * P, :], in_=win_sb[r % WINDOWS][:])
+            store(r)

@@ -63,9 +63,13 @@ def tile_list_hboth_silu_kernel(tc, xT, w_words, w_scales, wgt, b, wgo, offs, of
         wgt_sb = keep.tile([P, S], F32, name="wgt_sb", align_bytes=64)
         xb = {c.start: keep.tile([P, PASSES, width(c), PACK], BF16, name=f"xb{c.start}", align_bytes=64) for c in PIECES}
         xq = {c.start: keep.tile([P, PASSES, width(c)], U32, name=f"xq{c.start}", align_bytes=64) for c in PIECES}
-        xs = {c.start: keep.tile([P, PASSES, width(c)], U8, name=f"xs{c.start}", align_bytes=64) for c in PIECES}
+        xs_front = {c.start: keep.tile([P, PASSES * width(c)], U8, name=f"xs{c.start}", align_bytes=64) for c in PIECES[:2]}
+        xs1_last = keep.tile([P, width(LAST)], U8, name="xs1_last", align_bytes=64)
+        xs = {(c.start, a): xs_front[c.start][:, a * width(c) : (a + 1) * width(c)] for c in PIECES[:2] for a in range(PASSES)}
+        xs[LAST.start, 0] = xs_front[FIRST.start][SCALE_ROWS:P, :]
+        xs[LAST.start, 1] = xs1_last[:]
         w_sb = [keep.tile([P, PASSES, width(c)], I32, name=f"w{n}", align_bytes=64) for n, c in enumerate(W_CHUNKS)]
-        win_sb = [keep.tile([P, T], F32, name=f"win{n}") for n in range(WINDOWS - 1)]
+        win_sb = [keep.tile([P, T], F32, name=f"win{n}") for n in range(1)]
         ident = keep.tile([P, P], F32, name="ident")
         b_cols = keep.tile([P, ROW_TILES], F32, name="b_cols")
 
@@ -135,8 +139,15 @@ def tile_list_hboth_silu_kernel(tc, xT, w_words, w_scales, wgt, b, wgo, offs, of
         def quantize(piece):
             nc.vector.quantize_mx(
                 out=xq[piece.start][:].rearrange("p a s -> p (a s)").bitcast(FP8X4),
-                scales=xs[piece.start][:].rearrange("p a s -> p (a s)"),
+                scales=xs_front[piece.start][:],
                 in_=xb[piece.start][:].rearrange("p a s i -> p (a s i)"),
+            )
+
+        def quantize_last(a):
+            nc.vector.quantize_mx(
+                out=xq[LAST.start][:, a].bitcast(FP8X4),
+                scales=xs[LAST.start, a],
+                in_=xb[LAST.start][:, a].rearrange("p s i -> p (s i)"),
             )
 
         def multiply(r, part):
@@ -151,7 +162,7 @@ def tile_list_hboth_silu_kernel(tc, xT, w_words, w_scales, wgt, b, wgo, offs, of
                             lhsT=w_sb[n][:, a, col : col + P].bitcast(FP8X4),
                             lhsT_scale=ws_sb[r // 4][SCALE_ROWS * a : P, r % 4 * P : (r % 4 + 1) * P],
                             rhs=xq[piece.start][:, a].bitcast(FP8X4),
-                            rhs_scale=xs[piece.start][:, a],
+                            rhs_scale=xs[piece.start, a],
                             start=(a == 0),
                             stop=(a == PASSES - 1),
                         )
@@ -173,8 +184,9 @@ def tile_list_hboth_silu_kernel(tc, xT, w_words, w_scales, wgt, b, wgo, offs, of
                 gather(g0[:, i, part], 0, i, part)
         for piece in PIECES:
             interleave(nc.scalar.copy, xb[piece.start][:, 0], g0[:, :, piece])
-        win_sb.append(keep.tile([P, T], F32, name="win_last", tag="x0_0"))
-        nc.gpsimd.memset(win_sb[-1][:].bitcast(I32), 0)
+        for n in range(1, WINDOWS):
+            win_sb.append(keep.tile([P, T], F32, name=f"win{n}", tag=f"x0_{n - 1}"))
+            nc.gpsimd.memset(win_sb[n][:].bitcast(I32), 0)
         for i in range(2):
             gather(g1_row(i, WHOLE), 1, i, WHOLE)
         for piece in (FIRST, LAST):
@@ -182,21 +194,20 @@ def tile_list_hboth_silu_kernel(tc, xT, w_words, w_scales, wgt, b, wgo, offs, of
         gather(g1_row(2, FRONT), 1, 2, FRONT)
         gather(g1_row(3, FIRST), 1, 3, FIRST)
         gather(g1_row(3, MIDDLE), 1, 3, MIDDLE)
-        interleave(nc.vector.tensor_copy, xb[FIRST.start][:, 1, :, high], g1[:, high, FIRST])
-        third, fourth = slice(256, 384), slice(384, 512)
-        gather(g1_row(3, third), 1, 3, third)
+        interleave(nc.scalar.copy, xb[FIRST.start][:, 1, :, high], g1[:, high, FIRST])
+        gather(g1_row(3, LAST), 1, 3, LAST)
         quantize(FIRST)
         interleave(nc.scalar.copy, xb[MIDDLE.start][:, 1], g1[:, :, MIDDLE])
-        gather(g1_row(3, fourth), 1, 3, fourth)
         held = 3 * S + width(FIRST) - width(LAST)
         gather(g1_flat[:, held : held + width(LAST)], 1, 2, LAST)
         last_pair = g1_flat[:, PACK * S - 2 * width(REST) : PACK * S].rearrange("p (i s) -> p i s", i=2)
         quantize(MIDDLE)
         ys = [multiply(r, FIRST) for r in range(2)]
+        quantize_last(0)
         interleave(nc.scalar.copy, xb[LAST.start][:, 1, :, high], last_pair[:, :, width(FIRST) : width(REST)])
         scatter(0, FIRST, ys[0])
         scatter(1, FIRST, ys[1])
-        quantize(LAST)
+        quantize_last(1)
         scatter(2, FRONT, multiply(2, FRONT))
         for r in range(ROW_TILES):
             part = REST if r < 2 else LAST if r == 2 else WHOLE

@@ -24,6 +24,7 @@ EARLY = 3
 WINDOWS = EARLY
 FIRST_CHUNK_TILES = 2
 W_CHUNKS = (slice(0, FIRST_CHUNK_TILES * P), slice(FIRST_CHUNK_TILES * P, 4 * P), slice(4 * P, M))
+WS_CHUNKS = (W_CHUNKS[0], slice(W_CHUNKS[0].stop, M))
 
 F32 = mybir.dt.float32
 BF16 = mybir.dt.bfloat16
@@ -62,7 +63,11 @@ def tile_list_hboth_silu_kernel(tc, xT, w_words, w_scales, wgt, b, wgo, offs, of
         wgt_spread = keep.tile([P, S], F32, name="wgt_spread", align_bytes=64)
         wgt_sb = keep.tile([P, S], F32, name="wgt_sb", align_bytes=64)
         xb = {c.start: keep.tile([P, PASSES, width(c), PACK], BF16, name=f"xb{c.start}", align_bytes=64) for c in PIECES}
-        xq = {c.start: keep.tile([P, PASSES, width(c)], U32, name=f"xq{c.start}", align_bytes=64) for c in PIECES}
+        xq_back = {c.start: keep.tile([P, PASSES, width(c)], U32, name=f"xq{c.start}", align_bytes=64) for c in PIECES[1:]}
+        xq = {(c.start, a): xq_back[c.start][:, a] for c in PIECES[1:] for a in range(PASSES)}
+        xq1_first = keep.tile([P, width(FIRST)], U32, name="xq1_first", align_bytes=64)
+        xq[FIRST.start, 1] = xq1_first[:]
+        wgt_first = keep.tile([P, width(FIRST)], F32, name="wgt_first", align_bytes=64)
         xs_front = {c.start: keep.tile([P, PASSES * width(c)], U8, name=f"xs{c.start}", align_bytes=64) for c in PIECES[:2]}
         xs1_last = keep.tile([P, width(LAST)], U8, name="xs1_last", align_bytes=64)
         xs = {(c.start, a): xs_front[c.start][:, a * width(c) : (a + 1) * width(c)] for c in PIECES[:2] for a in range(PASSES)}
@@ -101,24 +106,24 @@ def tile_list_hboth_silu_kernel(tc, xT, w_words, w_scales, wgt, b, wgo, offs, of
         for part in (FRONT, LAST):
             nc.vector.transpose(wgt_sb[:, part], wgt_spread[:, part])
 
-        ws_sb = [keep.tile([P, M // 2], U8, name=f"ws{h}", align_bytes=64) for h in range(2)]
+        ws_sb = [keep.tile([P, width(c)], U8, name=f"ws{h}", align_bytes=64) for h, c in enumerate(WS_CHUNKS)]
         nc.scalar.activation(b_rows[0 : P - ROW_TILES, :], win_sb[0][0 : P - ROW_TILES, 0:P], SILU)
         make_identity(nc, ident[:])
         def load_scales(h):
-            cols = slice(h * M // 2, (h + 1) * M // 2)
+            cols = WS_CHUNKS[h]
             for q in range(P // SQUARE):
                 nc.sync.dma_start(
                     out=ws_sb[h][SQUARE * q : SQUARE * q + SCALE_ROWS * PASSES, :].bitcast(I32),
                     in_=w_scales[:, SCALE_ROWS * q : SCALE_ROWS * (q + 1), cols].bitcast(I32),
                 )
 
-        load_w(0)
         load_scales(0)
+        load_w(0)
         nc.sync.dma_start(out=wgo_sb[:, FIRST], in_=wgo[:, FIRST])
         nc.sync.dma_start(offs2_sb[:], offs2)
         load_w(1)
-        nc.sync.dma_start(out=wgo_sb[:, REST], in_=wgo[:, REST])
         load_scales(1)
+        nc.sync.dma_start(out=wgo_sb[:, REST], in_=wgo[:, REST])
         load_w(2)
 
         bank = psum.tile([P, P], F32, name="bank")
@@ -127,8 +132,11 @@ def tile_list_hboth_silu_kernel(tc, xT, w_words, w_scales, wgt, b, wgo, offs, of
         b_held = xb[LAST.start][:, 1].rearrange("p s i -> p (s i)").bitcast(F32)[:, 1:2]
         nc.scalar.copy(b_held, bank[:, P - ROW_TILES + 1 : P - ROW_TILES + 2])
 
-        def gather(products, a, i, part):
-            nc.vector.tensor_tensor(products, x_sb[a][i][:].indirect(offs_sb[:, columns(part)]), wgt_sb[:, part], MULT)
+        nc.scalar.copy(wgt_first[:], wgt_sb[:, FIRST])
+
+        def gather(products, a, i, part, weights=None):
+            weights = wgt_sb[:, part] if weights is None else weights
+            nc.vector.tensor_tensor(products, x_sb[a][i][:].indirect(offs_sb[:, columns(part)]), weights, MULT)
 
         def g1_row(i, part):
             return g1_flat[:, i * S + part.start : i * S + part.stop]
@@ -136,32 +144,34 @@ def tile_list_hboth_silu_kernel(tc, xT, w_words, w_scales, wgt, b, wgo, offs, of
         def interleave(copy, rounded, products):
             copy(rounded.rearrange("p (c e) i -> p c i e", e=4), products.rearrange("p i (c e) -> p c i e", e=4))
 
-        def quantize(piece):
+        def quantize_both(piece):
             nc.vector.quantize_mx(
-                out=xq[piece.start][:].rearrange("p a s -> p (a s)").bitcast(FP8X4),
+                out=xq_back[piece.start][:].rearrange("p a s -> p (a s)").bitcast(FP8X4),
                 scales=xs_front[piece.start][:],
                 in_=xb[piece.start][:].rearrange("p a s i -> p (a s i)"),
             )
 
-        def quantize_last(a):
+        def quantize(piece, a):
             nc.vector.quantize_mx(
-                out=xq[LAST.start][:, a].bitcast(FP8X4),
-                scales=xs[LAST.start, a],
-                in_=xb[LAST.start][:, a].rearrange("p s i -> p (s i)"),
+                out=xq[piece.start, a].bitcast(FP8X4),
+                scales=xs[piece.start, a],
+                in_=xb[piece.start][:, a].rearrange("p s i -> p (s i)"),
             )
 
         def multiply(r, part):
             acc = psum.tile([P, width(part)], F32, name="bank")
             n = [r * P < c.stop for c in W_CHUNKS].index(True)
             col = r * P - W_CHUNKS[n].start
+            h = min(n, 1)
+            scol = r * P - WS_CHUNKS[h].start
             for piece in PIECES:
                 if part.start <= piece.start < part.stop:
                     for a in range(PASSES):
                         nc.tensor.matmul_mx(
                             out=acc[:, piece.start - part.start : piece.stop - part.start],
                             lhsT=w_sb[n][:, a, col : col + P].bitcast(FP8X4),
-                            lhsT_scale=ws_sb[r // 4][SCALE_ROWS * a : P, r % 4 * P : (r % 4 + 1) * P],
-                            rhs=xq[piece.start][:, a].bitcast(FP8X4),
+                            lhsT_scale=ws_sb[h][SCALE_ROWS * a : P, scol : scol + P],
+                            rhs=xq[piece.start, a].bitcast(FP8X4),
                             rhs_scale=xs[piece.start, a],
                             start=(a == 0),
                             stop=(a == PASSES - 1),
@@ -191,25 +201,27 @@ def tile_list_hboth_silu_kernel(tc, xT, w_words, w_scales, wgt, b, wgo, offs, of
             gather(g1_row(i, WHOLE), 1, i, WHOLE)
         for piece in (FIRST, LAST):
             interleave(nc.scalar.copy, xb[piece.start][:, 1, :, low], g1[:, low, piece])
-        gather(g1_row(2, FRONT), 1, 2, FRONT)
-        gather(g1_row(3, FIRST), 1, 3, FIRST)
+        gather(g1_row(2, WHOLE), 1, 2, WHOLE)
+        gather(g1_flat[:, 3 * S + LAST.start : 3 * S + LAST.start + width(FIRST)], 1, 3, FIRST, wgt_first[:])
         gather(g1_row(3, MIDDLE), 1, 3, MIDDLE)
-        interleave(nc.scalar.copy, xb[FIRST.start][:, 1, :, high], g1[:, high, FIRST])
-        gather(g1_row(3, LAST), 1, 3, LAST)
-        quantize(FIRST)
+        first_pair = g1_flat[:, S:].rearrange("p (i s) -> p i s", i=2)[:, :, S : S + width(FIRST)]
+        interleave(nc.vector.tensor_copy, xb[FIRST.start][:, 1, :, high], first_pair)
+        xq0_first = keep.tile([P, width(FIRST)], U32, name="xq0_first", tag="wgt_first", align_bytes=64)
+        xq[FIRST.start, 0] = xq0_first[:]
+        quantize(FIRST, 0)
+        quantize(FIRST, 1)
         interleave(nc.scalar.copy, xb[MIDDLE.start][:, 1], g1[:, :, MIDDLE])
-        held = 3 * S + width(FIRST) - width(LAST)
-        gather(g1_flat[:, held : held + width(LAST)], 1, 2, LAST)
-        last_pair = g1_flat[:, PACK * S - 2 * width(REST) : PACK * S].rearrange("p (i s) -> p i s", i=2)
-        quantize(MIDDLE)
+        gather(g1_row(3, LAST), 1, 3, LAST)
+        quantize_both(MIDDLE)
         ys = [multiply(r, FIRST) for r in range(2)]
-        quantize_last(0)
-        interleave(nc.scalar.copy, xb[LAST.start][:, 1, :, high], last_pair[:, :, width(FIRST) : width(REST)])
+        quantize(LAST, 0)
+        interleave(nc.scalar.copy, xb[LAST.start][:, 1, :, high], g1[:, high, LAST])
         scatter(0, FIRST, ys[0])
         scatter(1, FIRST, ys[1])
-        quantize_last(1)
+        quantize(LAST, 1)
         scatter(2, FRONT, multiply(2, FRONT))
+        scatter(1, MIDDLE, multiply(1, MIDDLE))
         for r in range(ROW_TILES):
-            part = REST if r < 2 else LAST if r == 2 else WHOLE
+            part = REST if r == 0 else LAST if r < EARLY else WHOLE
             scatter(r, part, multiply(r, part))
             store(r)

@@ -21,7 +21,7 @@ WHOLE = slice(0, S)
 PIECES = (FIRST, MIDDLE, LAST)
 
 EARLY = 3
-WINDOWS = EARLY
+WINDOWS = EARLY + 1
 FIRST_CHUNK_TILES = 2
 W_CHUNKS = (slice(0, FIRST_CHUNK_TILES * P), slice(FIRST_CHUNK_TILES * P, 4 * P), slice(4 * P, M))
 WS_CHUNKS = (W_CHUNKS[0], slice(W_CHUNKS[0].stop, M))

@@ -62,17 +62,12 @@ def tile_list_hboth_silu_kernel(tc, xT, w_words, w_scales, wgt, b, wgo, offs, of
         wgt_turned = keep.tile([P, SQUARE], F32, name="wgt_turned", align_bytes=64)
         wgt_spread = keep.tile([P, S], F32, name="wgt_spread", align_bytes=64)
         wgt_sb = keep.tile([P, S], F32, name="wgt_sb", align_bytes=64)
-        xb = {c.start: keep.tile([P, PASSES, width(c), PACK], BF16, name=f"xb{c.start}", align_bytes=64) for c in PIECES}
-        xq_back = {c.start: keep.tile([P, PASSES, width(c)], U32, name=f"xq{c.start}", align_bytes=64) for c in PIECES[1:]}
-        xq = {(c.start, a): xq_back[c.start][:, a] for c in PIECES[1:] for a in range(PASSES)}
-        xq1_first = keep.tile([P, width(FIRST)], U32, name="xq1_first", align_bytes=64)
-        xq[FIRST.start, 1] = xq1_first[:]
+        calls = ((FRONT, 0), (LAST, 0), (FIRST, 1), (MIDDLE, 1), (LAST, 1))
+        xb = {(c.start, a): keep.tile([P, width(c), PACK], BF16, name=f"xb{a}_{c.start}", align_bytes=64) for c, a in calls}
+        xq = {(c.start, a): keep.tile([P, width(c)], U32, name=f"xq{a}_{c.start}", align_bytes=64) for c, a in calls[1:]}
+        xs = {(c.start, a): keep.tile([P, width(c)], U8, name=f"xs{a}_{c.start}", align_bytes=64)[:] for c, a in calls if (c, a) != (LAST, 0)}
+        xs[LAST.start, 0] = xs[FRONT.start, 0][SCALE_ROWS:P, :]
         wgt_first = keep.tile([P, width(FIRST)], F32, name="wgt_first", align_bytes=64)
-        xs_front = {c.start: keep.tile([P, PASSES * width(c)], U8, name=f"xs{c.start}", align_bytes=64) for c in PIECES[:2]}
-        xs1_last = keep.tile([P, width(LAST)], U8, name="xs1_last", align_bytes=64)
-        xs = {(c.start, a): xs_front[c.start][:, a * width(c) : (a + 1) * width(c)] for c in PIECES[:2] for a in range(PASSES)}
-        xs[LAST.start, 0] = xs_front[FIRST.start][SCALE_ROWS:P, :]
-        xs[LAST.start, 1] = xs1_last[:]
         w_sb = [keep.tile([P, PASSES, width(c)], I32, name=f"w{n}", align_bytes=64) for n, c in enumerate(W_CHUNKS)]
         win_sb = [keep.tile([P, T], F32, name=f"win{n}") for n in range(1)]
         ident = keep.tile([P, P], F32, name="ident")
@@ -129,7 +124,7 @@ def tile_list_hboth_silu_kernel(tc, xT, w_words, w_scales, wgt, b, wgo, offs, of
         bank = psum.tile([P, P], F32, name="bank")
         nc.tensor.transpose(bank[:], b_rows[:], ident[:])
         nc.scalar.copy(b_cols[:], bank[:, P - ROW_TILES : P])
-        b_held = xb[LAST.start][:, 1].rearrange("p s i -> p (s i)").bitcast(F32)[:, 1:2]
+        b_held = xb[LAST.start, 1][:].rearrange("p s i -> p (s i)").bitcast(F32)[:, 1:2]
         nc.scalar.copy(b_held, bank[:, P - ROW_TILES + 1 : P - ROW_TILES + 2])
 
         nc.scalar.copy(wgt_first[:], wgt_sb[:, FIRST])
@@ -144,19 +139,17 @@ def tile_list_hboth_silu_kernel(tc, xT, w_words, w_scales, wgt, b, wgo, offs, of
         def interleave(copy, rounded, products):
             copy(rounded.rearrange("p (c e) i -> p c i e", e=4), products.rearrange("p i (c e) -> p c i e", e=4))
 
-        def quantize_both(piece):
+        def quantize(part, a):
             nc.vector.quantize_mx(
-                out=xq_back[piece.start][:].rearrange("p a s -> p (a s)").bitcast(FP8X4),
-                scales=xs_front[piece.start][:],
-                in_=xb[piece.start][:].rearrange("p a s i -> p (a s i)"),
+                out=xq[part.start, a][:].bitcast(FP8X4),
+                scales=xs[part.start, a],
+                in_=xb[part.start, a][:].rearrange("p s i -> p (s i)"),
             )
 
-        def quantize(piece, a):
-            nc.vector.quantize_mx(
-                out=xq[piece.start, a].bitcast(FP8X4),
-                scales=xs[piece.start, a],
-                in_=xb[piece.start][:, a].rearrange("p s i -> p (s i)"),
-            )
+        def quantized(piece, a):
+            start = piece.start if (piece.start, a) in xq else FRONT.start
+            cols = slice(piece.start - start, piece.stop - start)
+            return xq[start, a][:, cols].bitcast(FP8X4), xs[start, a][:, cols]
 
         def multiply(r, part):
             acc = psum.tile([P, width(part)], F32, name="bank")
@@ -171,8 +164,8 @@ def tile_list_hboth_silu_kernel(tc, xT, w_words, w_scales, wgt, b, wgo, offs, of
                             out=acc[:, piece.start - part.start : piece.stop - part.start],
                             lhsT=w_sb[n][:, a, col : col + P].bitcast(FP8X4),
                             lhsT_scale=ws_sb[h][SCALE_ROWS * a : P, scol : scol + P],
-                            rhs=xq[piece.start, a].bitcast(FP8X4),
-                            rhs_scale=xs[piece.start, a],
+                            rhs=quantized(piece, a)[0],
+                            rhs_scale=quantized(piece, a)[1],
                             start=(a == 0),
                             stop=(a == PASSES - 1),
                         )
@@ -192,30 +185,33 @@ def tile_list_hboth_silu_kernel(tc, xT, w_words, w_scales, wgt, b, wgo, offs, of
         for i in range(PACK):
             for part in (FRONT, LAST) if i == 0 else (WHOLE,):
                 gather(g0[:, i, part], 0, i, part)
-        for piece in PIECES:
-            interleave(nc.scalar.copy, xb[piece.start][:, 0], g0[:, :, piece])
+            if i == 1:
+                interleave(nc.scalar.copy, xb[LAST.start, 0][:, :, low], g0[:, low, LAST])
+        interleave(nc.scalar.copy, xb[FRONT.start, 0][:], g0[:, :, FRONT])
+        interleave(nc.scalar.copy, xb[LAST.start, 0][:, :, high], g0[:, high, LAST])
         for n in range(1, WINDOWS):
             win_sb.append(keep.tile([P, T], F32, name=f"win{n}", tag=f"x0_{n - 1}"))
             nc.gpsimd.memset(win_sb[n][:].bitcast(I32), 0)
         for i in range(2):
             gather(g1_row(i, WHOLE), 1, i, WHOLE)
         for piece in (FIRST, LAST):
-            interleave(nc.scalar.copy, xb[piece.start][:, 1, :, low], g1[:, low, piece])
+            interleave(nc.scalar.copy, xb[piece.start, 1][:, :, low], g1[:, low, piece])
         gather(g1_row(2, WHOLE), 1, 2, WHOLE)
         gather(g1_flat[:, 3 * S + LAST.start : 3 * S + LAST.start + width(FIRST)], 1, 3, FIRST, wgt_first[:])
         gather(g1_row(3, MIDDLE), 1, 3, MIDDLE)
         first_pair = g1_flat[:, S:].rearrange("p (i s) -> p i s", i=2)[:, :, S : S + width(FIRST)]
-        interleave(nc.vector.tensor_copy, xb[FIRST.start][:, 1, :, high], first_pair)
-        xq0_first = keep.tile([P, width(FIRST)], U32, name="xq0_first", tag="wgt_first", align_bytes=64)
-        xq[FIRST.start, 0] = xq0_first[:]
-        quantize(FIRST, 0)
+        half = width(FIRST) // 2
+        interleave(nc.scalar.copy, xb[FIRST.start, 1][:, half:, high], first_pair[:, :, half:])
+        interleave(nc.vector.tensor_copy, xb[FIRST.start, 1][:, :half, high], first_pair[:, :, :half])
+        xq[FRONT.start, 0] = keep.tile([P, width(FRONT)], U32, name="xq0_front", tag="wgt_first", align_bytes=64)
+        quantize(FRONT, 0)
         quantize(FIRST, 1)
-        interleave(nc.scalar.copy, xb[MIDDLE.start][:, 1], g1[:, :, MIDDLE])
+        interleave(nc.scalar.copy, xb[MIDDLE.start, 1][:], g1[:, :, MIDDLE])
         gather(g1_row(3, LAST), 1, 3, LAST)
-        quantize_both(MIDDLE)
+        quantize(MIDDLE, 1)
         ys = [multiply(r, FIRST) for r in range(2)]
         quantize(LAST, 0)
-        interleave(nc.scalar.copy, xb[LAST.start][:, 1, :, high], g1[:, high, LAST])
+        interleave(nc.scalar.copy, xb[LAST.start, 1][:, :, high], g1[:, high, LAST])
         scatter(0, FIRST, ys[0])
         scatter(1, FIRST, ys[1])
         quantize(LAST, 1)

@@ -23,8 +23,8 @@ PIECES = (FIRST, MIDDLE, LAST)
 EARLY = 3
 WINDOWS = EARLY + 1
 FIRST_CHUNK_TILES = 2
-W_CHUNKS = (slice(0, FIRST_CHUNK_TILES * P), slice(FIRST_CHUNK_TILES * P, 4 * P), slice(4 * P, M))
-WS_CHUNKS = (W_CHUNKS[0], slice(W_CHUNKS[0].stop, M))
+W_CHUNKS = (slice(0, P), slice(P, 2 * P), slice(2 * P, 4 * P), slice(4 * P, M))
+WS_CHUNKS = (slice(0, FIRST_CHUNK_TILES * P), slice(FIRST_CHUNK_TILES * P, M))
 
 F32 = mybir.dt.float32
 BF16 = mybir.dt.bfloat16
@@ -114,12 +114,13 @@ def tile_list_hboth_silu_kernel(tc, xT, w_words, w_scales, wgt, b, wgo, offs, of
 
         load_scales(0)
         load_w(0)
+        load_w(1)
         nc.sync.dma_start(out=wgo_sb[:, FIRST], in_=wgo[:, FIRST])
         nc.sync.dma_start(offs2_sb[:], offs2)
-        load_w(1)
+        load_w(2)
         load_scales(1)
         nc.sync.dma_start(out=wgo_sb[:, REST], in_=wgo[:, REST])
-        load_w(2)
+        load_w(3)
 
         bank = psum.tile([P, P], F32, name="bank")
         nc.tensor.transpose(bank[:], b_rows[:], ident[:])
@@ -155,7 +156,7 @@ def tile_list_hboth_silu_kernel(tc, xT, w_words, w_scales, wgt, b, wgo, offs, of
             acc = psum.tile([P, width(part)], F32, name="bank")
             n = [r * P < c.stop for c in W_CHUNKS].index(True)
             col = r * P - W_CHUNKS[n].start
-            h = min(n, 1)
+            h = [r * P < c.stop for c in WS_CHUNKS].index(True)
             scol = r * P - WS_CHUNKS[h].start
             for piece in PIECES:
                 if part.start <= piece.start < part.stop:
@@ -196,22 +197,22 @@ def tile_list_hboth_silu_kernel(tc, xT, w_words, w_scales, wgt, b, wgo, offs, of
             gather(g1_row(i, WHOLE), 1, i, WHOLE)
         for piece in (FIRST, LAST):
             interleave(nc.scalar.copy, xb[piece.start, 1][:, :, low], g1[:, low, piece])
-        gather(g1_row(2, WHOLE), 1, 2, WHOLE)
-        gather(g1_flat[:, 3 * S + LAST.start : 3 * S + LAST.start + width(FIRST)], 1, 3, FIRST, wgt_first[:])
+        gather(g1_row(2, FRONT), 1, 2, FRONT)
+        gather(g1_row(3, FIRST), 1, 3, FIRST, wgt_first[:])
         gather(g1_row(3, MIDDLE), 1, 3, MIDDLE)
-        first_pair = g1_flat[:, S:].rearrange("p (i s) -> p i s", i=2)[:, :, S : S + width(FIRST)]
-        half = width(FIRST) // 2
-        interleave(nc.scalar.copy, xb[FIRST.start, 1][:, half:, high], first_pair[:, :, half:])
-        interleave(nc.vector.tensor_copy, xb[FIRST.start, 1][:, :half, high], first_pair[:, :, :half])
+        interleave(nc.scalar.copy, xb[FIRST.start, 1][:, :, high], g1[:, high, FIRST])
         xq[FRONT.start, 0] = keep.tile([P, width(FRONT)], U32, name="xq0_front", tag="wgt_first", align_bytes=64)
         quantize(FRONT, 0)
+        gather(g1_row(3, LAST), 1, 3, LAST)
         quantize(FIRST, 1)
         interleave(nc.scalar.copy, xb[MIDDLE.start, 1][:], g1[:, :, MIDDLE])
-        gather(g1_row(3, LAST), 1, 3, LAST)
+        held = 3 * S + width(FIRST) - width(LAST)
+        gather(g1_flat[:, held : held + width(LAST)], 1, 2, LAST)
+        last_pair = g1_flat[:, PACK * S - 2 * width(REST) : PACK * S].rearrange("p (i s) -> p i s", i=2)
         quantize(MIDDLE, 1)
         ys = [multiply(r, FIRST) for r in range(2)]
         quantize(LAST, 0)
-        interleave(nc.scalar.copy, xb[LAST.start, 1][:, :, high], g1[:, high, LAST])
+        interleave(nc.scalar.copy, xb[LAST.start, 1][:, :, high], last_pair[:, :, width(FIRST) : width(REST)])
         scatter(0, FIRST, ys[0])
         scatter(1, FIRST, ys[1])
         quantize(LAST, 1)

@@ -62,11 +62,23 @@ def tile_list_hboth_silu_kernel(tc, xT, w_words, w_scales, wgt, b, wgo, offs, of
         wgt_turned = keep.tile([P, SQUARE], F32, name="wgt_turned", align_bytes=64)
         wgt_spread = keep.tile([P, S], F32, name="wgt_spread", align_bytes=64)
         wgt_sb = keep.tile([P, S], F32, name="wgt_sb", align_bytes=64)
-        calls = ((FRONT, 0), (LAST, 0), (FIRST, 1), (MIDDLE, 1), (LAST, 1))
-        xb = {(c.start, a): keep.tile([P, width(c), PACK], BF16, name=f"xb{a}_{c.start}", align_bytes=64) for c, a in calls}
-        xq = {(c.start, a): keep.tile([P, width(c)], U32, name=f"xq{a}_{c.start}", align_bytes=64) for c, a in calls[1:]}
-        xs = {(c.start, a): keep.tile([P, width(c)], U8, name=f"xs{a}_{c.start}", align_bytes=64)[:] for c, a in calls if (c, a) != (LAST, 0)}
-        xs[LAST.start, 0] = xs[FRONT.start, 0][SCALE_ROWS:P, :]
+        xb = {
+            (c.start, a): keep.tile([P, width(c), PACK], BF16, name=f"xb{a}_{c.start}", align_bytes=64)[:]
+            for c in (FIRST, LAST)
+            for a in range(PASSES)
+        }
+        xs = {
+            (c.start, a): keep.tile([P, width(c)], U8, name=f"xs{a}_{c.start}", align_bytes=64)[:]
+            for c in (FIRST, LAST)
+            for a in range(PASSES)
+        }
+        xq = {(c.start, 1): keep.tile([P, width(c)], U32, name=f"xq1_{c.start}", align_bytes=64)[:] for c in (FIRST, LAST)}
+        xb_middle = keep.tile([P, PASSES * width(MIDDLE), PACK], BF16, name="xb_middle", align_bytes=64)
+        xq_middle = keep.tile([P, PASSES * width(MIDDLE)], U32, name="xq_middle", align_bytes=64)
+        xs_middle = keep.tile([P, PASSES * width(MIDDLE)], U8, name="xs_middle", align_bytes=64)
+        for a in range(PASSES):
+            cols = slice(a * width(MIDDLE), (a + 1) * width(MIDDLE))
+            xb[MIDDLE.start, a], xq[MIDDLE.start, a], xs[MIDDLE.start, a] = xb_middle[:, cols], xq_middle[:, cols], xs_middle[:, cols]
         wgt_first = keep.tile([P, width(FIRST)], F32, name="wgt_first", align_bytes=64)
         w_sb = [keep.tile([P, PASSES, width(c)], I32, name=f"w{n}", align_bytes=64) for n, c in enumerate(W_CHUNKS)]
         win_sb = [keep.tile([P, T], F32, name=f"win{n}") for n in range(1)]
@@ -125,7 +137,7 @@ def tile_list_hboth_silu_kernel(tc, xT, w_words, w_scales, wgt, b, wgo, offs, of
         bank = psum.tile([P, P], F32, name="bank")
         nc.tensor.transpose(bank[:], b_rows[:], ident[:])
         nc.scalar.copy(b_cols[:], bank[:, P - ROW_TILES : P])
-        b_held = xb[LAST.start, 1][:].rearrange("p s i -> p (s i)").bitcast(F32)[:, 1:2]
+        b_held = xb[LAST.start, 1].rearrange("p s i -> p (s i)").bitcast(F32)[:, 1:2]
         nc.scalar.copy(b_held, bank[:, P - ROW_TILES + 1 : P - ROW_TILES + 2])
 
         nc.scalar.copy(wgt_first[:], wgt_sb[:, FIRST])
@@ -140,17 +152,11 @@ def tile_list_hboth_silu_kernel(tc, xT, w_words, w_scales, wgt, b, wgo, offs, of
         def interleave(copy, rounded, products):
             copy(rounded.rearrange("p (c e) i -> p c i e", e=4), products.rearrange("p i (c e) -> p c i e", e=4))
 
-        def quantize(part, a):
-            nc.vector.quantize_mx(
-                out=xq[part.start, a][:].bitcast(FP8X4),
-                scales=xs[part.start, a],
-                in_=xb[part.start, a][:].rearrange("p s i -> p (s i)"),
-            )
+        def quantize(codes, scales, rounded):
+            nc.vector.quantize_mx(out=codes.bitcast(FP8X4), scales=scales, in_=rounded.rearrange("p s i -> p (s i)"))
 
-        def quantized(piece, a):
-            start = piece.start if (piece.start, a) in xq else FRONT.start
-            cols = slice(piece.start - start, piece.stop - start)
-            return xq[start, a][:, cols].bitcast(FP8X4), xs[start, a][:, cols]
+        def quantize_pass(piece, a):
+            quantize(xq[piece.start, a], xs[piece.start, a], xb[piece.start, a])
 
         def multiply(r, part):
             acc = psum.tile([P, width(part)], F32, name="bank")
@@ -165,8 +171,8 @@ def tile_list_hboth_silu_kernel(tc, xT, w_words, w_scales, wgt, b, wgo, offs, of
                             out=acc[:, piece.start - part.start : piece.stop - part.start],
                             lhsT=w_sb[n][:, a, col : col + P].bitcast(FP8X4),
                             lhsT_scale=ws_sb[h][SCALE_ROWS * a : P, scol : scol + P],
-                            rhs=quantized(piece, a)[0],
-                            rhs_scale=quantized(piece, a)[1],
+                            rhs=xq[piece.start, a].bitcast(FP8X4),
+                            rhs_scale=xs[piece.start, a],
                             start=(a == 0),
                             stop=(a == PASSES - 1),
                         )
@@ -186,39 +192,42 @@ def tile_list_hboth_silu_kernel(tc, xT, w_words, w_scales, wgt, b, wgo, offs, of
         for i in range(PACK):
             for part in (FRONT, LAST) if i == 0 else (WHOLE,):
                 gather(g0[:, i, part], 0, i, part)
-            if i == 1:
-                interleave(nc.scalar.copy, xb[LAST.start, 0][:, :, low], g0[:, low, LAST])
-        interleave(nc.scalar.copy, xb[FRONT.start, 0][:], g0[:, :, FRONT])
-        interleave(nc.scalar.copy, xb[LAST.start, 0][:, :, high], g0[:, high, LAST])
+            if i % 2 == 1:
+                for piece in PIECES:
+                    pair = slice(i - 1, i + 1)
+                    interleave(nc.scalar.copy, xb[piece.start, 0][:, :, pair], g0[:, pair, piece])
         for n in range(1, WINDOWS):
             win_sb.append(keep.tile([P, T], F32, name=f"win{n}", tag=f"x0_{n - 1}"))
             nc.gpsimd.memset(win_sb[n][:].bitcast(I32), 0)
-        for i in range(2):
-            gather(g1_row(i, WHOLE), 1, i, WHOLE)
-        for piece in (FIRST, LAST):
-            interleave(nc.scalar.copy, xb[piece.start, 1][:, :, low], g1[:, low, piece])
+        gather(g1_row(0, WHOLE), 1, 0, WHOLE)
+        gather(g1_row(1, LAST), 1, 1, LAST)
+        interleave(nc.scalar.copy, xb[LAST.start, 1][:, :, low], g1[:, low, LAST])
+        gather(g1_row(1, FRONT), 1, 1, FRONT)
+        interleave(nc.scalar.copy, xb[FIRST.start, 1][:, :, low], g1[:, low, FIRST])
         gather(g1_row(2, FRONT), 1, 2, FRONT)
         gather(g1_row(3, FIRST), 1, 3, FIRST, wgt_first[:])
         gather(g1_row(3, MIDDLE), 1, 3, MIDDLE)
         interleave(nc.scalar.copy, xb[FIRST.start, 1][:, :, high], g1[:, high, FIRST])
-        xq[FRONT.start, 0] = keep.tile([P, width(FRONT)], U32, name="xq0_front", tag="wgt_first", align_bytes=64)
-        quantize(FRONT, 0)
+        xq[FIRST.start, 0] = keep.tile([P, width(FIRST)], U32, name="xq0_first", tag="wgt_first", align_bytes=64)[:]
+        quantize_pass(FIRST, 0)
         gather(g1_row(3, LAST), 1, 3, LAST)
-        quantize(FIRST, 1)
-        interleave(nc.scalar.copy, xb[MIDDLE.start, 1][:], g1[:, :, MIDDLE])
+        quantize_pass(FIRST, 1)
+        interleave(nc.scalar.copy, xb[MIDDLE.start, 1], g1[:, :, MIDDLE])
         held = 3 * S + width(FIRST) - width(LAST)
         gather(g1_flat[:, held : held + width(LAST)], 1, 2, LAST)
         last_pair = g1_flat[:, PACK * S - 2 * width(REST) : PACK * S].rearrange("p (i s) -> p i s", i=2)
-        quantize(MIDDLE, 1)
+        quantize(xq_middle[:], xs_middle[:], xb_middle[:])
+        xq[LAST.start, 0] = keep.tile([P, width(LAST)], U32, name="xq0_last", tag="xb1_0", align_bytes=64)[:]
+        quantize_pass(LAST, 0)
         ys = [multiply(r, FIRST) for r in range(2)]
-        quantize(LAST, 0)
         interleave(nc.scalar.copy, xb[LAST.start, 1][:, :, high], last_pair[:, :, width(FIRST) : width(REST)])
         scatter(0, FIRST, ys[0])
         scatter(1, FIRST, ys[1])
-        quantize(LAST, 1)
         scatter(2, FRONT, multiply(2, FRONT))
+        quantize_pass(LAST, 1)
+        scatter(3, FRONT, multiply(3, FRONT))
         scatter(1, MIDDLE, multiply(1, MIDDLE))
         for r in range(ROW_TILES):
-            part = REST if r == 0 else LAST if r < EARLY else WHOLE
+            part = REST if r == 0 else LAST if r < WINDOWS else WHOLE
             scatter(r, part, multiply(r, part))
             store(r)

@@ -21,9 +21,9 @@ WHOLE = slice(0, S)
 PIECES = (FIRST, MIDDLE, LAST)
 
 EARLY = 3
-WINDOWS = EARLY + 1
+WINDOWS = EARLY
 FIRST_CHUNK_TILES = 2
-W_CHUNKS = (slice(0, P), slice(P, 2 * P), slice(2 * P, 4 * P), slice(4 * P, M))
+W_CHUNKS = (slice(0, P), slice(P, 2 * P), slice(2 * P, 3 * P), slice(3 * P, M))
 WS_CHUNKS = (slice(0, FIRST_CHUNK_TILES * P), slice(FIRST_CHUNK_TILES * P, M))
 
 F32 = mybir.dt.float32
@@ -62,23 +62,12 @@ def tile_list_hboth_silu_kernel(tc, xT, w_words, w_scales, wgt, b, wgo, offs, of
         wgt_turned = keep.tile([P, SQUARE], F32, name="wgt_turned", align_bytes=64)
         wgt_spread = keep.tile([P, S], F32, name="wgt_spread", align_bytes=64)
         wgt_sb = keep.tile([P, S], F32, name="wgt_sb", align_bytes=64)
-        xb = {
-            (c.start, a): keep.tile([P, width(c), PACK], BF16, name=f"xb{a}_{c.start}", align_bytes=64)[:]
-            for c in (FIRST, LAST)
-            for a in range(PASSES)
-        }
-        xs = {
-            (c.start, a): keep.tile([P, width(c)], U8, name=f"xs{a}_{c.start}", align_bytes=64)[:]
-            for c in (FIRST, LAST)
-            for a in range(PASSES)
-        }
-        xq = {(c.start, 1): keep.tile([P, width(c)], U32, name=f"xq1_{c.start}", align_bytes=64)[:] for c in (FIRST, LAST)}
-        xb_middle = keep.tile([P, PASSES * width(MIDDLE), PACK], BF16, name="xb_middle", align_bytes=64)
-        xq_middle = keep.tile([P, PASSES * width(MIDDLE)], U32, name="xq_middle", align_bytes=64)
-        xs_middle = keep.tile([P, PASSES * width(MIDDLE)], U8, name="xs_middle", align_bytes=64)
-        for a in range(PASSES):
-            cols = slice(a * width(MIDDLE), (a + 1) * width(MIDDLE))
-            xb[MIDDLE.start, a], xq[MIDDLE.start, a], xs[MIDDLE.start, a] = xb_middle[:, cols], xq_middle[:, cols], xs_middle[:, cols]
+        xb0 = keep.tile([P, S, PACK], BF16, name="xb0", align_bytes=64)
+        xb1 = {c.start: keep.tile([P, width(c), PACK], BF16, name=f"xb1_{c.start}", align_bytes=64)[:] for c in PIECES}
+        xq = {(c.start, 1): keep.tile([P, width(c)], U32, name=f"xq1_{c.start}", align_bytes=64)[:] for c in PIECES}
+        xs = {(c.start, 1): keep.tile([P, width(c)], U8, name=f"xs1_{c.start}", align_bytes=64)[:] for c in PIECES}
+        xs[FIRST.start, 0] = keep.tile([P, width(FIRST)], U8, name="xs0_first", align_bytes=64)[:]
+        xs0_rest = keep.tile([P, width(REST)], U8, name="xs0_rest", align_bytes=64)
         wgt_first = keep.tile([P, width(FIRST)], F32, name="wgt_first", align_bytes=64)
         w_sb = [keep.tile([P, PASSES, width(c)], I32, name=f"w{n}", align_bytes=64) for n, c in enumerate(W_CHUNKS)]
         win_sb = [keep.tile([P, T], F32, name=f"win{n}") for n in range(1)]
@@ -137,7 +126,7 @@ def tile_list_hboth_silu_kernel(tc, xT, w_words, w_scales, wgt, b, wgo, offs, of
         bank = psum.tile([P, P], F32, name="bank")
         nc.tensor.transpose(bank[:], b_rows[:], ident[:])
         nc.scalar.copy(b_cols[:], bank[:, P - ROW_TILES : P])
-        b_held = xb[LAST.start, 1].rearrange("p s i -> p (s i)").bitcast(F32)[:, 1:2]
+        b_held = xb1[LAST.start].rearrange("p s i -> p (s i)").bitcast(F32)[:, 1:2]
         nc.scalar.copy(b_held, bank[:, P - ROW_TILES + 1 : P - ROW_TILES + 2])
 
         nc.scalar.copy(wgt_first[:], wgt_sb[:, FIRST])
@@ -149,14 +138,14 @@ def tile_list_hboth_silu_kernel(tc, xT, w_words, w_scales, wgt, b, wgo, offs, of
         def g1_row(i, part):
             return g1_flat[:, i * S + part.start : i * S + part.stop]
 
-        def interleave(copy, rounded, products):
-            copy(rounded.rearrange("p (c e) i -> p c i e", e=4), products.rearrange("p i (c e) -> p c i e", e=4))
+        def interleave(rounded, products):
+            nc.scalar.copy(rounded.rearrange("p (c e) i -> p c i e", e=4), products.rearrange("p i (c e) -> p c i e", e=4))
 
         def quantize(codes, scales, rounded):
             nc.vector.quantize_mx(out=codes.bitcast(FP8X4), scales=scales, in_=rounded.rearrange("p s i -> p (s i)"))
 
-        def quantize_pass(piece, a):
-            quantize(xq[piece.start, a], xs[piece.start, a], xb[piece.start, a])
+        def quantize_pass1(piece):
+            quantize(xq[piece.start, 1], xs[piece.start, 1], xb1[piece.start])
 
         def multiply(r, part):
             acc = psum.tile([P, width(part)], F32, name="bank")
@@ -193,41 +182,39 @@ def tile_list_hboth_silu_kernel(tc, xT, w_words, w_scales, wgt, b, wgo, offs, of
             for part in (FRONT, LAST) if i == 0 else (WHOLE,):
                 gather(g0[:, i, part], 0, i, part)
             if i % 2 == 1:
-                for piece in PIECES:
-                    pair = slice(i - 1, i + 1)
-                    interleave(nc.scalar.copy, xb[piece.start, 0][:, :, pair], g0[:, pair, piece])
+                pair = slice(i - 1, i + 1)
+                interleave(xb0[:, :, pair], g0[:, pair, :])
         for n in range(1, WINDOWS):
             win_sb.append(keep.tile([P, T], F32, name=f"win{n}", tag=f"x0_{n - 1}"))
             nc.gpsimd.memset(win_sb[n][:].bitcast(I32), 0)
         gather(g1_row(0, WHOLE), 1, 0, WHOLE)
-        gather(g1_row(1, LAST), 1, 1, LAST)
-        interleave(nc.scalar.copy, xb[LAST.start, 1][:, :, low], g1[:, low, LAST])
-        gather(g1_row(1, FRONT), 1, 1, FRONT)
-        interleave(nc.scalar.copy, xb[FIRST.start, 1][:, :, low], g1[:, low, FIRST])
+        interleave(xb1[FIRST.start][:, :, 0:1], g1[:, 0:1, FIRST])
+        gather(g1_row(1, WHOLE), 1, 1, WHOLE)
+        interleave(xb1[LAST.start][:, :, low], g1[:, low, LAST])
         gather(g1_row(2, FRONT), 1, 2, FRONT)
         gather(g1_row(3, FIRST), 1, 3, FIRST, wgt_first[:])
-        gather(g1_row(3, MIDDLE), 1, 3, MIDDLE)
-        interleave(nc.scalar.copy, xb[FIRST.start, 1][:, :, high], g1[:, high, FIRST])
+        gather(g1_row(3, REST), 1, 3, REST)
+        interleave(xb1[FIRST.start][:, :, 1:PACK], g1[:, 1:PACK, FIRST])
         xq[FIRST.start, 0] = keep.tile([P, width(FIRST)], U32, name="xq0_first", tag="wgt_first", align_bytes=64)[:]
-        quantize_pass(FIRST, 0)
-        gather(g1_row(3, LAST), 1, 3, LAST)
-        quantize_pass(FIRST, 1)
-        interleave(nc.scalar.copy, xb[MIDDLE.start, 1], g1[:, :, MIDDLE])
+        quantize(xq[FIRST.start, 0], xs[FIRST.start, 0], xb0[:, FIRST])
+        quantize_pass1(FIRST)
+        interleave(xb1[MIDDLE.start], g1[:, :, MIDDLE])
         held = 3 * S + width(FIRST) - width(LAST)
         gather(g1_flat[:, held : held + width(LAST)], 1, 2, LAST)
         last_pair = g1_flat[:, PACK * S - 2 * width(REST) : PACK * S].rearrange("p (i s) -> p i s", i=2)
-        quantize(xq_middle[:], xs_middle[:], xb_middle[:])
-        xq[LAST.start, 0] = keep.tile([P, width(LAST)], U32, name="xq0_last", tag="xb1_0", align_bytes=64)[:]
-        quantize_pass(LAST, 0)
+        xq0_rest = keep.tile([P, width(REST)], U32, name="xq0_rest", tag="xb1_0", align_bytes=64)
+        quantize(xq0_rest[:], xs0_rest[:], xb0[:, REST])
+        for c in (MIDDLE, LAST):
+            cols = slice(c.start - REST.start, c.stop - REST.start)
+            xq[c.start, 0], xs[c.start, 0] = xq0_rest[:, cols], xs0_rest[:, cols]
+        quantize_pass1(MIDDLE)
         ys = [multiply(r, FIRST) for r in range(2)]
-        interleave(nc.scalar.copy, xb[LAST.start, 1][:, :, high], last_pair[:, :, width(FIRST) : width(REST)])
+        interleave(xb1[LAST.start][:, :, high], last_pair[:, :, width(FIRST) : width(REST)])
         scatter(0, FIRST, ys[0])
         scatter(1, FIRST, ys[1])
+        quantize_pass1(LAST)
         scatter(2, FRONT, multiply(2, FRONT))
-        quantize_pass(LAST, 1)
-        scatter(3, FRONT, multiply(3, FRONT))
-        scatter(1, MIDDLE, multiply(1, MIDDLE))
         for r in range(ROW_TILES):
-            part = REST if r == 0 else LAST if r < WINDOWS else WHOLE
+            part = REST if r < 2 else LAST if r < WINDOWS else WHOLE
             scatter(r, part, multiply(r, part))
             store(r)

@@ -26,6 +26,8 @@ FIRST_CHUNK_TILES = 2
 W_CHUNKS = (slice(0, P), slice(P, 2 * P), slice(2 * P, 3 * P), slice(3 * P, M))
 WS_CHUNKS = (slice(0, FIRST_CHUNK_TILES * P), slice(FIRST_CHUNK_TILES * P, M))
 
+AXI = 256
+
 F32 = mybir.dt.float32
 BF16 = mybir.dt.bfloat16
 I32 = mybir.dt.int32
@@ -53,8 +55,8 @@ def tile_list_hboth_silu_kernel(tc, xT, w_words, w_scales, wgt, b, wgo, offs, of
 
         offs_sb = keep.tile([P, S // GROUP], U16, name="offs_sb")
         offs2_sb = keep.tile([P, S // GROUP], U16, name="offs2_sb")
-        wgo_sb = keep.tile([P, S], F32, name="wgo_sb")
-        x_sb = [[keep.tile([P, T], F32, name=f"x{a}_{i}") for i in range(PACK)] for a in range(PASSES)]
+        wgo_sb = keep.tile([P, S], F32, name="wgo_sb", align_bytes=AXI)
+        x_sb = [[keep.tile([P, T], F32, name=f"x{a}_{i}", align_bytes=AXI) for i in range(PACK)] for a in range(PASSES)]
         g0 = keep.tile([P, PACK, S], F32, name="g0")
         g1_flat = keep.tile([P, PACK * S], F32, name="g1_flat", align_bytes=64)
         g1 = g1_flat[:].rearrange("p (i s) -> p i s", i=PACK)
@@ -69,8 +71,8 @@ def tile_list_hboth_silu_kernel(tc, xT, w_words, w_scales, wgt, b, wgo, offs, of
         xs[FIRST.start, 0] = keep.tile([P, width(FIRST)], U8, name="xs0_first", align_bytes=64)[:]
         xs0_rest = keep.tile([P, width(REST)], U8, name="xs0_rest", align_bytes=64)
         wgt_first = keep.tile([P, width(FIRST)], F32, name="wgt_first", align_bytes=64)
-        w_sb = [keep.tile([P, PASSES, width(c)], I32, name=f"w{n}", align_bytes=64) for n, c in enumerate(W_CHUNKS)]
-        win_sb = [keep.tile([P, T], F32, name=f"win{n}") for n in range(1)]
+        w_sb = [keep.tile([P, PASSES, width(c)], I32, name=f"w{n}", align_bytes=AXI) for n, c in enumerate(W_CHUNKS)]
+        win_sb = [keep.tile([P, T], F32, name=f"win{n}", align_bytes=AXI) for n in range(1)]
         ident = keep.tile([P, P], F32, name="ident")
         b_cols = keep.tile([P, ROW_TILES], F32, name="b_cols")
 
@@ -185,7 +187,7 @@ def tile_list_hboth_silu_kernel(tc, xT, w_words, w_scales, wgt, b, wgo, offs, of
                 pair = slice(i - 1, i + 1)
                 interleave(xb0[:, :, pair], g0[:, pair, :])
         for n in range(1, WINDOWS):
-            win_sb.append(keep.tile([P, T], F32, name=f"win{n}", tag=f"x0_{n - 1}"))
+            win_sb.append(keep.tile([P, T], F32, name=f"win{n}", tag=f"x0_{n - 1}", align_bytes=AXI))
             nc.gpsimd.memset(win_sb[n][:].bitcast(I32), 0)
         gather(g1_row(0, WHOLE), 1, 0, WHOLE)
         interleave(xb1[FIRST.start][:, :, 0:1], g1[:, 0:1, FIRST])

@@ -72,7 +72,7 @@ def tile_list_hboth_silu_kernel(tc, xT, w_words, w_scales, wgt, b, wgo, offs, of
         xs0_rest = keep.tile([P, width(REST)], U8, name="xs0_rest", align_bytes=64)
         wgt_first = keep.tile([P, width(FIRST)], F32, name="wgt_first", align_bytes=64)
         w_sb = [keep.tile([P, PASSES, width(c)], I32, name=f"w{n}", align_bytes=AXI) for n, c in enumerate(W_CHUNKS)]
-        win_sb = [keep.tile([P, T], F32, name=f"win{n}", align_bytes=AXI) for n in range(1)]
+        win_sb = [keep.tile([P, T], F32, name=f"win{n}", align_bytes=AXI) for n in range(2)]
         ident = keep.tile([P, P], F32, name="ident")
         b_cols = keep.tile([P, ROW_TILES], F32, name="b_cols")
 
@@ -186,8 +186,8 @@ def tile_list_hboth_silu_kernel(tc, xT, w_words, w_scales, wgt, b, wgo, offs, of
             if i % 2 == 1:
                 pair = slice(i - 1, i + 1)
                 interleave(xb0[:, :, pair], g0[:, pair, :])
-        for n in range(1, WINDOWS):
-            win_sb.append(keep.tile([P, T], F32, name=f"win{n}", tag=f"x0_{n - 1}", align_bytes=AXI))
+        for n in range(2, WINDOWS):
+            win_sb.append(keep.tile([P, T], F32, name=f"win{n}", tag=f"x0_{n - 2}", align_bytes=AXI))
             nc.gpsimd.memset(win_sb[n][:].bitcast(I32), 0)
         gather(g1_row(0, WHOLE), 1, 0, WHOLE)
         interleave(xb1[FIRST.start][:, :, 0:1], g1[:, 0:1, FIRST])

@@ -104,16 +104,14 @@ def tile_list_hboth_silu_kernel(tc, xT, w_words, w_scales, wgt, b, wgo, offs, of
         for part in (FRONT, LAST):
             nc.vector.transpose(wgt_sb[:, part], wgt_spread[:, part])
 
-        ws_sb = [keep.tile([P, width(c)], U8, name=f"ws{h}", align_bytes=64) for h, c in enumerate(WS_CHUNKS)]
+        ws_sb = [keep.tile([P, PASSES, width(c)], U8, name=f"ws{h}", align_bytes=64) for h, c in enumerate(WS_CHUNKS)]
+        ws_view = w_scales.rearrange("a (q r) n -> r q a n", r=SCALE_ROWS)
         nc.scalar.activation(b_rows[0 : P - ROW_TILES, :], win_sb[0][0 : P - ROW_TILES, 0:P], SILU)
         make_identity(nc, ident[:])
         def load_scales(h):
             cols = WS_CHUNKS[h]
-            for q in range(P // SQUARE):
-                nc.sync.dma_start(
-                    out=ws_sb[h][SQUARE * q : SQUARE * q + SCALE_ROWS * PASSES, :].bitcast(I32),
-                    in_=w_scales[:, SCALE_ROWS * q : SCALE_ROWS * (q + 1), cols].bitcast(I32),
-                )
+            for r in range(SCALE_ROWS):
+                nc.sync.dma_start(out=ws_sb[h][r:P:SQUARE].bitcast(I32), in_=ws_view[r, :, :, cols].bitcast(I32))
 
         load_scales(0)
         load_w(0)
@@ -161,7 +159,7 @@ def tile_list_hboth_silu_kernel(tc, xT, w_words, w_scales, wgt, b, wgo, offs, of
                         nc.tensor.matmul_mx(
                             out=acc[:, piece.start - part.start : piece.stop - part.start],
                             lhsT=w_sb[n][:, a, col : col + P].bitcast(FP8X4),
-                            lhsT_scale=ws_sb[h][SCALE_ROWS * a : P, scol : scol + P],
+                            lhsT_scale=ws_sb[h][:, a, scol : scol + P],
                             rhs=xq[piece.start, a].bitcast(FP8X4),
                             rhs_scale=xs[piece.start, a],
                             start=(a == 0),

from contextlib import ExitStack

import concourse.mybir as mybir
from concourse.masks import make_identity

K, M, T, S = 1024, 1024, 1024, 512
FLOPS = 2 * K * M * S

P = 128
PACK = 4
PASSES = K // (P * PACK)
ROW_TILES = M // P
SQUARE = 32
SCALE_ROWS = 4
GROUP = 16

FIRST, MIDDLE, LAST = slice(0, 128), slice(128, 256), slice(256, S)
FRONT = slice(FIRST.start, MIDDLE.stop)
REST = slice(MIDDLE.start, LAST.stop)
WHOLE = slice(0, S)
PIECES = (FIRST, MIDDLE, LAST)

EARLY = 3
WINDOWS = EARLY
FIRST_CHUNK_TILES = 2
W_CHUNKS = (slice(0, P), slice(P, 2 * P), slice(2 * P, 3 * P), slice(3 * P, M))
WS_CHUNKS = (slice(0, FIRST_CHUNK_TILES * P), slice(FIRST_CHUNK_TILES * P, M))

AXI = 256

F32 = mybir.dt.float32
BF16 = mybir.dt.bfloat16
I32 = mybir.dt.int32
U32 = mybir.dt.uint32
U16 = mybir.dt.uint16
U8 = mybir.dt.uint8
FP8X4 = mybir.dt.float8_e4m3fn_x4
MULT = mybir.AluOpType.mult
SILU = mybir.ActivationFunctionType.Silu


def width(part):
    return part.stop - part.start


def columns(part):
    return slice(part.start // GROUP, part.stop // GROUP)


def tile_list_hboth_silu_kernel(tc, xT, w_words, w_scales, wgt, b, wgo, offs, offs2, out):
    nc = tc.nc
    with ExitStack() as ctx:
        keep = ctx.enter_context(tc.tile_pool(name="keep", bufs=1))
        psum = ctx.enter_context(tc.psum_pool(name="psum", bufs=8))

        offs_sb = keep.tile([P, S // GROUP], U16, name="offs_sb")
        offs2_sb = keep.tile([P, S // GROUP], U16, name="offs2_sb")
        wgo_sb = keep.tile([P, S], F32, name="wgo_sb", align_bytes=AXI)
        x_sb = [[keep.tile([P, T], F32, name=f"x{a}_{i}", align_bytes=AXI) for i in range(PACK)] for a in range(PASSES)]
        g0 = keep.tile([P, PACK, S], F32, name="g0")
        g1_flat = keep.tile([P, PACK * S], F32, name="g1_flat", align_bytes=64)
        g1 = g1_flat[:].rearrange("p (i s) -> p i s", i=PACK)
        wgt_dealt = keep.tile([P, SQUARE], F32, name="wgt_dealt", align_bytes=64)
        wgt_turned = keep.tile([P, SQUARE], F32, name="wgt_turned", align_bytes=64)
        wgt_spread = keep.tile([P, S], F32, name="wgt_spread", align_bytes=64)
        wgt_sb = keep.tile([P, S], F32, name="wgt_sb", align_bytes=64)
        xb0 = keep.tile([P, S, PACK], BF16, name="xb0", align_bytes=64)
        xb1 = {c.start: keep.tile([P, width(c), PACK], BF16, name=f"xb1_{c.start}", align_bytes=64)[:] for c in PIECES}
        xq = {(c.start, 1): keep.tile([P, width(c)], U32, name=f"xq1_{c.start}", align_bytes=64)[:] for c in PIECES}
        xs = {(c.start, 1): keep.tile([P, width(c)], U8, name=f"xs1_{c.start}", align_bytes=64)[:] for c in PIECES}
        xs[FIRST.start, 0] = keep.tile([P, width(FIRST)], U8, name="xs0_first", align_bytes=64)[:]
        xs0_rest = keep.tile([P, width(REST)], U8, name="xs0_rest", align_bytes=64)
        wgt_first = keep.tile([P, width(FIRST)], F32, name="wgt_first", align_bytes=64)
        w_sb = [keep.tile([P, PASSES, width(c)], I32, name=f"w{n}", align_bytes=AXI) for n, c in enumerate(W_CHUNKS)]
        win_sb = [keep.tile([P, T], F32, name=f"win{n}", align_bytes=AXI) for n in range(2)]
        ident = keep.tile([P, P], F32, name="ident")
        b_cols = keep.tile([P, ROW_TILES], F32, name="b_cols")

        x_view = xT.rearrange("(a p i) t -> a i p t", p=P, i=PACK)
        w_view = w_words.rearrange("a p n t -> p a (n t)")

        def load_w(n):
            c = W_CHUNKS[n]
            nc.sync.dma_start(out=w_sb[n][:], in_=w_view[:, :, PACK * c.start : PACK * c.stop].bitcast(I32))

        nc.scalar.dma_start(out=wgt_dealt[:], in_=wgt.rearrange("(g q) (r c) -> g q r c", q=GROUP, c=SQUARE)[:, 0])
        b_rows = keep.tile([P, P], F32, name="b_rows", align_bytes=64)
        nc.scalar.dma_start(out=b_rows[P - ROW_TILES : P, :], in_=b.rearrange("(r p) -> r p", p=P))
        nc.sync.dma_start(offs_sb[:], offs)
        for a in range(PASSES):
            for i in range(PACK):
                nc.sync.dma_start(out=x_sb[a][i][:], in_=x_view[a, i])

        for window in win_sb:
            nc.vector.memset(window[:].bitcast(I32), 0)

        nc.vector.transpose(wgt_turned[:], wgt_dealt[:])
        spread = wgt_spread[:].rearrange("p (r h q) -> p r h q", h=SQUARE // GROUP, q=GROUP)
        turned = wgt_turned[:].rearrange("p (h r) -> p r h", r=GROUP)
        for rows in (slice(0, GROUP // 2), slice(GROUP // 2, GROUP)):
            nc.vector.tensor_copy(
                spread[:, rows], turned[:, rows].unsqueeze(3).to_broadcast([P, GROUP // 2, SQUARE // GROUP, GROUP])
            )
        for part in (FRONT, LAST):
            nc.vector.transpose(wgt_sb[:, part], wgt_spread[:, part])

        ws_sb = [keep.tile([P, PASSES, width(c)], U8, name=f"ws{h}", align_bytes=64) for h, c in enumerate(WS_CHUNKS)]
        ws_view = w_scales.rearrange("a (q r) n -> r q a n", r=SCALE_ROWS)
        nc.scalar.activation(b_rows[0 : P - ROW_TILES, :], win_sb[0][0 : P - ROW_TILES, 0:P], SILU)
        make_identity(nc, ident[:])
        def load_scales(h):
            cols = WS_CHUNKS[h]
            for r in range(SCALE_ROWS):
                nc.sync.dma_start(out=ws_sb[h][r:P:SQUARE].bitcast(I32), in_=ws_view[r, :, :, cols].bitcast(I32))

        load_scales(0)
        load_w(0)
        load_w(1)
        nc.sync.dma_start(out=wgo_sb[:, FIRST], in_=wgo[:, FIRST])
        nc.sync.dma_start(offs2_sb[:], offs2)
        load_w(2)
        load_scales(1)
        nc.sync.dma_start(out=wgo_sb[:, REST], in_=wgo[:, REST])
        load_w(3)

        bank = psum.tile([P, P], F32, name="bank")
        nc.tensor.transpose(bank[:], b_rows[:], ident[:])
        nc.scalar.copy(b_cols[:], bank[:, P - ROW_TILES : P])
        b_held = xb1[LAST.start].rearrange("p s i -> p (s i)").bitcast(F32)[:, 1:2]
        nc.scalar.copy(b_held, bank[:, P - ROW_TILES + 1 : P - ROW_TILES + 2])

        nc.scalar.copy(wgt_first[:], wgt_sb[:, FIRST])

        def gather(products, a, i, part, weights=None):
            weights = wgt_sb[:, part] if weights is None else weights
            nc.vector.tensor_tensor(products, x_sb[a][i][:].indirect(offs_sb[:, columns(part)]), weights, MULT)

        def g1_row(i, part):
            return g1_flat[:, i * S + part.start : i * S + part.stop]

        def interleave(rounded, products):
            nc.scalar.copy(rounded.rearrange("p (c e) i -> p c i e", e=4), products.rearrange("p i (c e) -> p c i e", e=4))

        def quantize(codes, scales, rounded):
            nc.vector.quantize_mx(out=codes.bitcast(FP8X4), scales=scales, in_=rounded.rearrange("p s i -> p (s i)"))

        def quantize_pass1(piece):
            quantize(xq[piece.start, 1], xs[piece.start, 1], xb1[piece.start])

        def multiply(r, part):
            acc = psum.tile([P, width(part)], F32, name="bank")
            n = [r * P < c.stop for c in W_CHUNKS].index(True)
            col = r * P - W_CHUNKS[n].start
            h = [r * P < c.stop for c in WS_CHUNKS].index(True)
            scol = r * P - WS_CHUNKS[h].start
            for piece in PIECES:
                if part.start <= piece.start < part.stop:
                    for a in range(PASSES):
                        nc.tensor.matmul_mx(
                            out=acc[:, piece.start - part.start : piece.stop - part.start],
                            lhsT=w_sb[n][:, a, col : col + P].bitcast(FP8X4),
                            lhsT_scale=ws_sb[h][:, a, scol : scol + P],
                            rhs=xq[piece.start, a].bitcast(FP8X4),
                            rhs_scale=xs[piece.start, a],
                            start=(a == 0),
                            stop=(a == PASSES - 1),
                        )
            y = keep.tile([P, width(part)], F32, name=f"y{r}_{part.start}")
            nc.scalar.activation(y[:], acc[:], SILU, bias=b_held if (r, part) == (1, FIRST) else b_cols[:, r : r + 1])
            return y

        def scatter(r, part, y):
            nc.vector.tensor_tensor(
                win_sb[r % WINDOWS][:].indirect(offs2_sb[:, columns(part)]), y[:], wgo_sb[:, part], MULT
            )

        def store(r):
            nc.sync.dma_start(out=out[r * P : (r + 1) * P, :], in_=win_sb[r % WINDOWS][:])

        low, high = slice(0, 2), slice(2, 4)
        for i in range(PACK):
            for part in (FRONT, LAST) if i == 0 else (WHOLE,):
                gather(g0[:, i, part], 0, i, part)
            if i % 2 == 1:
                pair = slice(i - 1, i + 1)
                interleave(xb0[:, :, pair], g0[:, pair, :])
        for n in range(2, WINDOWS):
            win_sb.append(keep.tile([P, T], F32, name=f"win{n}", tag=f"x0_{n - 2}", align_bytes=AXI))
            nc.gpsimd.memset(win_sb[n][:].bitcast(I32), 0)
        gather(g1_row(0, WHOLE), 1, 0, WHOLE)
        interleave(xb1[FIRST.start][:, :, 0:1], g1[:, 0:1, FIRST])
        gather(g1_row(1, WHOLE), 1, 1, WHOLE)
        interleave(xb1[LAST.start][:, :, low], g1[:, low, LAST])
        gather(g1_row(2, FRONT), 1, 2, FRONT)
        gather(g1_row(3, FIRST), 1, 3, FIRST, wgt_first[:])
        gather(g1_row(3, REST), 1, 3, REST)
        interleave(xb1[FIRST.start][:, :, 1:PACK], g1[:, 1:PACK, FIRST])
        xq[FIRST.start, 0] = keep.tile([P, width(FIRST)], U32, name="xq0_first", tag="wgt_first", align_bytes=64)[:]
        quantize(xq[FIRST.start, 0], xs[FIRST.start, 0], xb0[:, FIRST])
        quantize_pass1(FIRST)
        interleave(xb1[MIDDLE.start], g1[:, :, MIDDLE])
        held = 3 * S + width(FIRST) - width(LAST)
        gather(g1_flat[:, held : held + width(LAST)], 1, 2, LAST)
        last_pair = g1_flat[:, PACK * S - 2 * width(REST) : PACK * S].rearrange("p (i s) -> p i s", i=2)
        xq0_rest = keep.tile([P, width(REST)], U32, name="xq0_rest", tag="xb1_0", align_bytes=64)
        quantize(xq0_rest[:], xs0_rest[:], xb0[:, REST])
        for c in (MIDDLE, LAST):
            cols = slice(c.start - REST.start, c.stop - REST.start)
            xq[c.start, 0], xs[c.start, 0] = xq0_rest[:, cols], xs0_rest[:, cols]
        quantize_pass1(MIDDLE)
        ys = [multiply(r, FIRST) for r in range(2)]
        interleave(xb1[LAST.start][:, :, high], last_pair[:, :, width(FIRST) : width(REST)])
        scatter(0, FIRST, ys[0])
        scatter(1, FIRST, ys[1])
        quantize_pass1(LAST)
        scatter(2, FRONT, multiply(2, FRONT))
        for r in range(ROW_TILES):
            part = REST if r < 2 else LAST if r < WINDOWS else WHOLE
            scatter(r, part, multiply(r, part))
            store(r)
